import numpy as np
import ml_dtypes


def mxq(x, axis, fmt="e4m3"):
    dtype, down = {"e4m3": (ml_dtypes.float8_e4m3fn, 7), "e5m2": (ml_dtypes.float8_e5m2, 14)}[fmt]
    v = np.moveaxis(np.asarray(x, np.float32).astype(ml_dtypes.bfloat16).astype(np.float64), axis, -1)
    blocks = v.reshape(v.shape[:-1] + (-1, 32))
    amax = np.abs(blocks).max(-1, keepdims=True)
    byte = np.maximum(np.where(amax > 0, np.frexp(amax)[1] - 1 + 127, 0) - down, 1)
    scale = np.exp2(byte - 127.0)
    codes = (blocks / scale).astype(np.float32).astype(dtype).astype(np.float64)
    return np.moveaxis((codes * scale).reshape(v.shape), -1, axis)


WIDE = False


def mx_kscale(k):
    if not WIDE:
        return np.ones(k)
    levels = np.array([10, -10, 5, -5, 0])
    if k % 512:
        return np.exp2(np.random.permutation(np.resize(levels, k // 32))).repeat(32)
    a = np.empty((k // 512, 16))
    for p in range(k // 512):
        a[p, :8] = np.random.permutation(np.resize(levels, 8))
        for g in range(8):
            far = levels[np.abs(levels - a[p, g]) >= 10]
            a[p, g + 8] = far[np.random.randint(len(far))]
    return np.exp2(a.ravel()).repeat(32)


def f64(x):
    return np.asarray(x).astype(np.float64)


def striped(idx):
    return np.tile(idx.reshape(-1, 16).T, (8, 1)).astype(np.uint16)


def unstriped(offs):
    return offs[:16].T.reshape(-1).astype(np.int64)


def pack_weight(w):
    k, n = w.shape
    w = f64(np.asarray(w, np.float32).astype(ml_dtypes.bfloat16)).reshape(k // 32, 32, n)
    amax = np.abs(w).max(1)
    byte = np.clip(np.where(amax > 0, np.frexp(amax)[1] - 1 + 127 - 7, 1), 1, 254)
    scaled = (w * np.exp2(127.0 - byte)[:, None, :]).reshape(k, n).astype(np.float32)
    words = np.ascontiguousarray(scaled.reshape(k // 512, 128, 4, n).transpose(0, 1, 3, 2)).astype(ml_dtypes.float8_e4m3fn).view(np.uint8)
    return words, np.ascontiguousarray(byte.astype(np.uint8).reshape(k // 512, 16, n))


def unpack_weight(words, scales):
    g, p, n, _ = words.shape
    vals = np.ascontiguousarray(words).view(ml_dtypes.float8_e4m3fn).astype(np.float64) * np.repeat(np.exp2(scales.astype(np.float64) - 127.0), 8, axis=1)[..., None]
    return vals.transpose(0, 1, 3, 2).reshape(g * 512, n)


def planes(y):
    n, m = y.shape
    v = y.astype(np.float32).astype(ml_dtypes.bfloat16).astype(np.float64).reshape(n // 32, 32, m)
    top = np.abs(v).max(1)
    byte = np.clip(np.where(top > 0, np.frexp(top)[1] - 1 + 127 - 7, 1), 1, 254)
    codes = (v * np.exp2(127.0 - byte)[:, None, :]).reshape(n, m).astype(np.float32).astype(ml_dtypes.float8_e4m3fn).view(np.uint8)
    words = codes.reshape(n // 512, 128, 4, m).transpose(0, 1, 3, 2)
    return np.ascontiguousarray(words), np.ascontiguousarray(byte.astype(np.uint8).reshape(n // 512, 16, m))


def sigmoid(v):
    return 1.0 / (1.0 + np.exp(-np.maximum(v, -700.0)))


K, T, S, W, N = 512, 1024, 512, 1024, 512


def setup_inputs():
    n = np.random.standard_normal
    s = mx_kscale(K)[:, None]
    packed_xT = pack_weight(n((K, T)) * s)
    packed_eT = pack_weight(n((K, W)) * s)
    return {
        "x_words": packed_xT[0],
        "x_scales": packed_xT[1],
        "e_words": packed_eT[0],
        "e_scales": packed_eT[1],
        "w1": (n((K, N)) / np.sqrt(2 * K) / s).astype(np.float32),
        "v1": (n((K, N)) / np.sqrt(2 * K) / s).astype(np.float32),
        "w2": (n((K, N)) / np.sqrt(2 * K) / s).astype(np.float32),
        "w3": (n((K, N)) / np.sqrt(2 * K) / s).astype(np.float32),
        "v3": (n((K, N)) / np.sqrt(2 * K) / s).astype(np.float32),
        "carry": (n((N, T))).astype(np.float32),
        "offs": striped(np.random.permutation(T)[:S]),
        "tok": striped(np.random.permutation(W)[:S]),
    }


def reference(x_words, x_scales, e_words, e_scales, w1, v1, w2, w3, v3, carry, offs, tok):
    old = f64(carry)[:, unstriped(offs)]
    xq = unpack_weight(x_words, x_scales)[:, unstriped(offs)]
    e_tok = unpack_weight(e_words, e_scales)[:, unstriped(tok)]
    z = sigmoid(mxq(f64(w1), 0, "e4m3").T @ xq + mxq(f64(v1), 0, "e4m3").T @ e_tok)
    r = sigmoid(mxq(f64(w2), 0, "e4m3").T @ xq)
    g = np.tanh((mxq(f64(v3), 0, "e4m3").T @ e_tok) + r * ((mxq(f64(w3), 0, "e4m3").T @ xq)))
    out_0 = old + z * (g - old)
    return (out_0,) + planes(out_0)

@@ -1,0 +1,214 @@
+from contextlib import ExitStack
+
+import concourse.mybir as mybir
+
+FLOPS = 5 * 2 * 512 * 512 * 512
+
+F32 = mybir.dt.float32
+BF16 = mybir.dt.bfloat16
+I32 = mybir.dt.int32
+U32 = mybir.dt.uint32
+U16 = mybir.dt.uint16
+U8 = mybir.dt.uint8
+FP8X4 = mybir.dt.float8_e4m3fn_x4
+ADD = mybir.AluOpType.add
+SUB = mybir.AluOpType.subtract
+MULT = mybir.AluOpType.mult
+TANH = mybir.ActivationFunctionType.Tanh
+
+P = 128
+PACK = 4
+S = 512
+T = 1024
+N = 512
+HALF = S // 2
+
+
+def tile_picked_zgru_gru_po_kernel(
+    tc, x_words, x_scales, e_words, e_scales, w1, v1, w2, w3, v3, carry, offs, tok, out_0, out_1, out_2
+):
+    nc = tc.nc
+    with ExitStack() as ctx:
+        lists = ctx.enter_context(tc.tile_pool(name="lists", bufs=1))
+        sb = ctx.enter_context(tc.tile_pool(name="sb", bufs=1))
+        laid = ctx.enter_context(tc.tile_pool(name="laid", bufs=1))
+        psum = ctx.enter_context(tc.psum_pool(name="psum", bufs=1))
+
+        offs_t = lists.tile([P, S // 16], U16, name="offs_t")
+        tok_t = lists.tile([P, S // 16], U16, name="tok_t")
+
+        def tl(shape, dt, name, tag=None):
+            return sb.tile(shape, dt, name=name, tag=tag or name, align_bytes=64)
+
+        def at(shape, dt, name, offset):
+            return laid.tile(shape, dt, name=name, align_bytes=64, offset=offset)
+
+        warm_in = tl([P, 1], F32, "warm_in")
+        warm_out = tl([P, 1], F32, "warm_out")
+        nc.vector.memset(warm_in[:], 0.0)
+        nc.scalar.activation(warm_out[:], warm_in[:], TANH)
+
+        xs_tab = tl([P, T], U8, "xs_tab")
+        es_tab = tl([P, T], U8, "es_tab")
+        nc.gpsimd.memset(xs_tab[:].bitcast(I32), 0)
+        nc.gpsimd.memset(es_tab[:].bitcast(I32), 0)
+
+        def load_scales(src, tab):
+            for q in range(4):
+                nc.sync.dma_start(tab[32 * q : 32 * q + 4, :].bitcast(I32), src[0, 4 * q : 4 * q + 4, :].bitcast(I32))
+
+        def load_words(src, name):
+            tab = tl([P, T], I32, name)
+            nc.sync.dma_start(tab[:], src[0].rearrange("p n t -> p (n t)").bitcast(I32))
+            return tab
+
+        def load_weight(w, name, tag):
+            raw = tl([P, PACK, N], F32, name, tag)
+            nc.sync.dma_start(raw[:], w.rearrange("(p j) c -> p j c", j=PACK))
+            return raw
+
+        def load_carry(t, tag):
+            tab = tl([P, T], F32, "carry%d" % t, tag)
+            nc.sync.dma_start(tab[:], carry.rearrange("(p t) c -> p t c", t=PACK)[:, t, :])
+            return tab
+
+        def cast(raw, grouped, vector_cols):
+            dst = grouped[:].rearrange("p (t m j) -> p m j t", t=PACK, j=PACK)
+            src = raw[:].rearrange("p j (m t) -> p m j t", t=PACK)
+            if vector_cols > 0:
+                nc.vector.tensor_copy(dst[:, :, :, 0:vector_cols], src[:, :, :, 0:vector_cols])
+            if vector_cols < PACK:
+                nc.scalar.copy(dst[:, :, :, vector_cols:PACK], src[:, :, :, vector_cols:PACK])
+
+        def quant(grouped, name):
+            codes = tl([P, N], U32, name + "_codes")
+            scales = tl([P, N], U8, name + "_scales")
+            nc.vector.quantize_mx(out=codes[:].bitcast(FP8X4), scales=scales[:], in_=grouped[:])
+            return codes, scales
+
+        def gather_packed(wtab, stab, lst, words, scales):
+            nc.vector.tensor_copy(words[:], wtab[:].bitcast(U32).indirect(lst[:]))
+            nc.vector.tensor_copy(scales[:], stab[:].indirect(lst[:]))
+            return words, scales
+
+        def gather_carry(tab, dst):
+            nc.vector.tensor_copy(dst[:], tab[:].indirect(offs_t[:]))
+            return dst
+
+        def bank(b, name):
+            return psum.tile([P, S], F32, name=name, tag="bank%d" % b)
+
+        def mm(acc, wq, aq, t, start, stop):
+            cols = slice(t * P, (t + 1) * P)
+            nc.tensor.matmul_mx(
+                out=acc[:],
+                lhsT=wq[0][:, cols].bitcast(FP8X4),
+                lhsT_scale=wq[1][:, cols],
+                rhs=aq[0][:].bitcast(FP8X4),
+                rhs_scale=aq[1][:],
+                start=start,
+                stop=stop,
+            )
+
+        xw_tab = load_words(x_words, "xw_tab")
+        nc.sync.dma_start(offs_t[:], offs)
+        nc.sync.dma_start(tok_t[:], tok)
+        load_scales(x_scales, xs_tab)
+        w2_raw = load_weight(w2, "w2_raw", "raw_a")
+        ew_tab = load_words(e_words, "ew_tab")
+        load_scales(e_scales, es_tab)
+        w3_raw = load_weight(w3, "w3_raw", "raw_b")
+
+        xq = gather_packed(xw_tab, xs_tab, offs_t, tl([P, S], U32, "x_words_g"), tl([P, S], U8, "x_scales_g"))
+        carry0 = load_carry(0, "xw_tab")
+        w2_g = at([P, PACK * N], BF16, "w2_g", 0)
+        cast(w2_raw, w2_g, 2)
+        v3_raw = load_weight(v3, "v3_raw", "raw_a")
+        w2_q = quant(w2_g, "w2")
+        r_ps = [bank(t, "r_ps%d" % t) for t in range(PACK)]
+        for t in range(PACK):
+            mm(r_ps[t], w2_q, xq, t, True, True)
+        eq = gather_packed(ew_tab, es_tab, tok_t, at([P, S], U32, "e_words_g", 0), at([P, S], U8, "e_scales_g", 2048))
+        carry1 = load_carry(1, "ew_tab")
+        w3_g = at([P, PACK * N], BF16, "w3_g", 2560)
+        cast(w3_raw, w3_g, 2)
+        w1_raw = load_weight(w1, "w1_raw", "raw_b")
+        tr = [tl([P, S], F32, "tr%d" % t) for t in range(PACK)]
+        for t in range(PACK):
+            nc.scalar.activation(tr[t][:], r_ps[t][:], TANH, scale=0.5)
+        w3_q = quant(w3_g, "w3")
+        d_ps = [bank(4 + t, "d_ps%d" % t) for t in range(PACK)]
+        for t in range(PACK):
+            mm(d_ps[t], w3_q, xq, t, True, True)
+        old = [gather_carry(carry0, at([P, S], F32, "old0", 4608))]
+        v1_raw = load_weight(v1, "v1_raw", "xw_tab")
+        v3_g = tl([P, PACK * N], BF16, "v3_g")
+        cast(v3_raw, v3_g, 0)
+        u = [tl([P, S], F32, "u%d" % t) for t in range(PACK)]
+        for t in range(PACK):
+            nc.vector.scalar_tensor_tensor(u[t][:], tr[t][:], 1.0, d_ps[t][:], ADD, MULT)
+        carry2 = load_carry(2, "tr0")
+        carry3 = load_carry(3, "tr1")
+        v3_q = quant(v3_g, "v3")
+        old.append(gather_carry(carry1, tl([P, S], F32, "old1", "tr3")))
+        c_ps = [bank(t, "c_ps%d" % t) for t in range(PACK)]
+        for t in range(PACK):
+            mm(c_ps[t], v3_q, eq, t, True, True)
+        w1_g = tl([P, PACK * N], BF16, "w1_g")
+        cast(w1_raw, w1_g, 0)
+        v1_g = at([P, PACK * N], BF16, "v1_g", 8192)
+        cast(v1_raw, v1_g, 0)
+        v = [tl([P, S], F32, "v%d" % t) for t in range(PACK)]
+        for t in range(PACK):
+            nc.vector.scalar_tensor_tensor(v[t][:], u[t][:], 0.5, c_ps[t][:], MULT, ADD)
+        w1_q = quant(w1_g, "w1")
+        z_ps = [bank(4 + t, "z_ps%d" % t) for t in range(PACK)]
+        for t in range(PACK):
+            mm(z_ps[t], w1_q, xq, t, True, False)
+        g = tl([P, PACK, S], F32, "g")
+        for t in range(PACK):
+            nc.scalar.activation(g[:, t, :], v[t][:], TANH)
+        v1_q = quant(v1_g, "v1")
+        for t in range(PACK):
+            mm(z_ps[t], v1_q, eq, t, False, True)
+        old.append(gather_carry(carry2, at([P, S], F32, "old2", 8192)))
+        old.append(gather_carry(carry3, at([P, S], F32, "old3", 10240)))
+        d = tl([P, PACK, S], F32, "d")
+        for t in range(PACK):
+            engine = nc.gpsimd if t in [] else nc.vector
+            engine.tensor_tensor(d[:, t, :], g[:, t, :], old[t][:], SUB)
+
+        y_codes = tl([P, S], U32, "y_codes")
+        y_scales = tl([P, S], U8, "y_scales")
+        out_rows = out_0.rearrange("(p t) c -> p t c", t=PACK)
+        out_words = out_1[0].rearrange("p n t -> p (n t)").bitcast(I32)
+        tz = tl([P, PACK, S], F32, "tz")
+        e = tl([P, PACK, S], F32, "e")
+        y = tl([P, PACK, S], F32, "y")
+        yb = [tl([P, HALF, PACK], BF16, "yb%d" % h) for h in range(2)]
+        for h in range(2):
+            cols = slice(h * HALF, (h + 1) * HALF)
+            for t in range(PACK):
+                nc.scalar.activation(tz[:, t, cols], z_ps[t][:, cols], TANH, scale=0.5)
+        for h in range(2):
+            cols = slice(h * HALF, (h + 1) * HALF)
+            for a in range(0, PACK, 2):
+                nc.vector.scalar_tensor_tensor(e[:, a : a + 2, cols], tz[:, a : a + 2, cols], 1.0, d[:, a : a + 2, cols], ADD, MULT)
+            for t in range(PACK):
+                nc.vector.scalar_tensor_tensor(y[:, t, cols], e[:, t, cols], 0.5, old[t][:, cols], MULT, ADD)
+            nc.sync.dma_start(out_rows[:, :, cols], y[:, :, cols])
+            dst = yb[h][:].rearrange("p (c i) t -> p c t i", i=4)
+            src = y[:, :, cols].rearrange("p t (c i) -> p c t i", i=4)
+            vec = 0 if h == 0 else 40
+            if vec > 0:
+                nc.vector.tensor_copy(dst[:, 0:vec], src[:, 0:vec])
+            nc.scalar.copy(dst[:, vec:], src[:, vec:])
+        for h in range(2):
+            cols = slice(h * HALF, (h + 1) * HALF)
+            nc.vector.quantize_mx(
+                out=y_codes[:, cols].bitcast(FP8X4), scales=y_scales[:, cols], in_=yb[h][:].rearrange("p c t -> p (c t)")
+            )
+            nc.sync.dma_start(out_words[:, cols], y_codes[:, cols].bitcast(I32))
+        for q in range(4):
+            queue = nc.scalar if q % 2 else nc.sync
+            queue.dma_start(out_2[0, 4 * q : 4 * q + 4, :].bitcast(I32), y_scales[32 * q : 32 * q + 4, :].bitcast(I32))

@@ -51,7 +51,7 @@ def tile_picked_zgru_gru_po_kernel(
         xs_tab = tl([P, T], U8, "xs_tab")
         es_tab = tl([P, T], U8, "es_tab")
         nc.gpsimd.memset(xs_tab[:].bitcast(I32), 0)
-        nc.gpsimd.memset(es_tab[:].bitcast(I32), 0)
+        nc.vector.memset(es_tab[:].bitcast(I32), 0)
 
         def load_scales(src, tab):
             for q in range(4):
@@ -72,13 +72,17 @@ def tile_picked_zgru_gru_po_kernel(
             nc.sync.dma_start(tab[:], carry.rearrange("(p t) c -> p t c", t=PACK)[:, t, :])
             return tab
 
-        def cast(raw, grouped, vector_cols):
+        def cast(raw, grouped, helper):
             dst = grouped[:].rearrange("p (t m j) -> p m j t", t=PACK, j=PACK)
             src = raw[:].rearrange("p j (m t) -> p m j t", t=PACK)
-            if vector_cols > 0:
-                nc.vector.tensor_copy(dst[:, :, :, 0:vector_cols], src[:, :, :, 0:vector_cols])
-            if vector_cols < PACK:
-                nc.scalar.copy(dst[:, :, :, vector_cols:PACK], src[:, :, :, vector_cols:PACK])
+            if helper == "v":
+                nc.vector.tensor_copy(dst[:, :, :, 0:2], src[:, :, :, 0:2])
+            if helper == "g":
+                nc.gpsimd.tensor_scalar(dst[:, :, :, 0:2], src[:, :, :, 0:2], 1.0, 0.0, MULT, ADD)
+            if helper == "s":
+                nc.scalar.copy(dst, src)
+            else:
+                nc.scalar.copy(dst[:, :, :, 2:PACK], src[:, :, :, 2:PACK])
 
         def quant(grouped, name):
             codes = tl([P, N], U32, name + "_codes")
@@ -112,26 +116,31 @@ def tile_picked_zgru_gru_po_kernel(
 
         xw_tab = load_words(x_words, "xw_tab")
         nc.sync.dma_start(offs_t[:], offs)
-        nc.sync.dma_start(tok_t[:], tok)
+        carry0 = load_carry(0, "carry0")
         load_scales(x_scales, xs_tab)
         w2_raw = load_weight(w2, "w2_raw", "raw_a")
+        nc.sync.dma_start(tok_t[:], tok)
         ew_tab = load_words(e_words, "ew_tab")
         load_scales(e_scales, es_tab)
         w3_raw = load_weight(w3, "w3_raw", "raw_b")
 
-        xq = gather_packed(xw_tab, xs_tab, offs_t, tl([P, S], U32, "x_words_g"), tl([P, S], U8, "x_scales_g"))
-        carry0 = load_carry(0, "xw_tab")
+        x_words_g = tl([P, S], U32, "x_words_g")
+        x_scales_g = tl([P, S], U8, "x_scales_g")
+        nc.vector.tensor_copy(x_words_g[:], xw_tab[:].bitcast(U32).indirect(offs_t[:]))
+        carry1 = load_carry(1, "xw_tab")
+        old = [gather_carry(carry0, tl([P, S], F32, "old0"))]
+        nc.vector.tensor_copy(x_scales_g[:], xs_tab[:].indirect(offs_t[:]))
+        xq = (x_words_g, x_scales_g)
         w2_g = at([P, PACK * N], BF16, "w2_g", 0)
-        cast(w2_raw, w2_g, 2)
+        cast(w2_raw, w2_g, "v")
         v3_raw = load_weight(v3, "v3_raw", "raw_a")
         w2_q = quant(w2_g, "w2")
         r_ps = [bank(t, "r_ps%d" % t) for t in range(PACK)]
         for t in range(PACK):
             mm(r_ps[t], w2_q, xq, t, True, True)
         eq = gather_packed(ew_tab, es_tab, tok_t, at([P, S], U32, "e_words_g", 0), at([P, S], U8, "e_scales_g", 2048))
-        carry1 = load_carry(1, "ew_tab")
         w3_g = at([P, PACK * N], BF16, "w3_g", 2560)
-        cast(w3_raw, w3_g, 2)
+        cast(w3_raw, w3_g, "v")
         w1_raw = load_weight(w1, "w1_raw", "raw_b")
         tr = [tl([P, S], F32, "tr%d" % t) for t in range(PACK)]
         for t in range(PACK):
@@ -140,24 +149,21 @@ def tile_picked_zgru_gru_po_kernel(
         d_ps = [bank(4 + t, "d_ps%d" % t) for t in range(PACK)]
         for t in range(PACK):
             mm(d_ps[t], w3_q, xq, t, True, True)
-        old = [gather_carry(carry0, at([P, S], F32, "old0", 4608))]
+        old.append(gather_carry(carry1, at([P, S], F32, "old1", 4608)))
         v1_raw = load_weight(v1, "v1_raw", "xw_tab")
-        v3_g = tl([P, PACK * N], BF16, "v3_g")
-        cast(v3_raw, v3_g, 0)
+        v3_g = at([P, PACK * N], BF16, "v3_g", 8192)
+        cast(v3_raw, v3_g, "s")
         u = [tl([P, S], F32, "u%d" % t) for t in range(PACK)]
         for t in range(PACK):
             nc.vector.scalar_tensor_tensor(u[t][:], tr[t][:], 1.0, d_ps[t][:], ADD, MULT)
         carry2 = load_carry(2, "tr0")
         carry3 = load_carry(3, "tr1")
         v3_q = quant(v3_g, "v3")
-        old.append(gather_carry(carry1, tl([P, S], F32, "old1", "tr3")))
         c_ps = [bank(t, "c_ps%d" % t) for t in range(PACK)]
         for t in range(PACK):
             mm(c_ps[t], v3_q, eq, t, True, True)
-        w1_g = tl([P, PACK * N], BF16, "w1_g")
-        cast(w1_raw, w1_g, 0)
-        v1_g = at([P, PACK * N], BF16, "v1_g", 8192)
-        cast(v1_raw, v1_g, 0)
+        w1_g = at([P, PACK * N], BF16, "w1_g", 12288)
+        cast(w1_raw, w1_g, "s")
         v = [tl([P, S], F32, "v%d" % t) for t in range(PACK)]
         for t in range(PACK):
             nc.vector.scalar_tensor_tensor(v[t][:], u[t][:], 0.5, c_ps[t][:], MULT, ADD)
@@ -166,16 +172,18 @@ def tile_picked_zgru_gru_po_kernel(
         for t in range(PACK):
             mm(z_ps[t], w1_q, xq, t, True, False)
         g = tl([P, PACK, S], F32, "g")
+        v1_g = at([P, PACK * N], BF16, "v1_g", 16384)
+        cast(v1_raw, v1_g, "s")
         for t in range(PACK):
             nc.scalar.activation(g[:, t, :], v[t][:], TANH)
         v1_q = quant(v1_g, "v1")
         for t in range(PACK):
             mm(z_ps[t], v1_q, eq, t, False, True)
-        old.append(gather_carry(carry2, at([P, S], F32, "old2", 8192)))
-        old.append(gather_carry(carry3, at([P, S], F32, "old3", 10240)))
+        old.append(gather_carry(carry2, at([P, S], F32, "old2", 16384)))
+        old.append(gather_carry(carry3, at([P, S], F32, "old3", 18432)))
         d = tl([P, PACK, S], F32, "d")
         for t in range(PACK):
-            engine = nc.gpsimd if t in [] else nc.vector
+            engine = nc.gpsimd if t in [0,1] else nc.vector
             engine.tensor_tensor(d[:, t, :], g[:, t, :], old[t][:], SUB)
 
         y_codes = tl([P, S], U32, "y_codes")

@@ -53,9 +53,9 @@ def tile_picked_zgru_gru_po_kernel(
         nc.gpsimd.memset(xs_tab[:].bitcast(I32), 0)
         nc.vector.memset(es_tab[:].bitcast(I32), 0)
 
-        def load_scales(src, tab):
+        def load_scales(src, tab, row):
             for q in range(4):
-                nc.sync.dma_start(tab[32 * q : 32 * q + 4, :].bitcast(I32), src[0, 4 * q : 4 * q + 4, :].bitcast(I32))
+                nc.sync.dma_start(tab[32 * q + row : 32 * q + row + 4, :].bitcast(I32), src[0, 4 * q : 4 * q + 4, :].bitcast(I32))
 
         def load_words(src, name):
             tab = tl([P, T], I32, name)
@@ -84,20 +84,29 @@ def tile_picked_zgru_gru_po_kernel(
             else:
                 nc.scalar.copy(dst[:, :, :, 2:PACK], src[:, :, :, 2:PACK])
 
-        def quant(grouped, name):
-            codes = tl([P, N], U32, name + "_codes")
+        def quant(grouped, name, tag=None):
+            codes = tl([P, N], U32, name + "_codes", tag)
             scales = tl([P, N], U8, name + "_scales")
             nc.vector.quantize_mx(out=codes[:].bitcast(FP8X4), scales=scales[:], in_=grouped[:])
+            return codes, scales
+
+        def shared_cast_quant(raw, lo, hi, name):
+            src = raw[:].rearrange("p j (m t) -> p m j t", t=PACK)
+            nc.vector.tensor_copy(lo[:].rearrange("p (t m j) -> p m j t", t=2, j=PACK), src[:, :, :, 0:2])
+            nc.scalar.copy(hi[:].rearrange("p (t m j) -> p m j t", t=2, j=PACK), src[:, :, :, 2:PACK])
+            codes = tl([P, N], U32, name + "_codes")
+            scales = tl([P, N], U8, name + "_scales")
+            for cols, half in ((slice(0, N // 2), lo), (slice(N // 2, N), hi)):
+                nc.vector.quantize_mx(out=codes[:, cols].bitcast(FP8X4), scales=scales[:, cols], in_=half[:])
             return codes, scales
 
         def gather_packed(wtab, stab, lst, words, scales):
             nc.vector.tensor_copy(words[:], wtab[:].bitcast(U32).indirect(lst[:]))
             nc.vector.tensor_copy(scales[:], stab[:].indirect(lst[:]))
-            return words, scales
+            return words, scales[4:P, :]
 
         def gather_carry(tab, dst):
-            nc.vector.tensor_copy(dst[:], tab[:].indirect(offs_t[:]))
-            return dst
+            nc.vector.tensor_copy(dst, tab[:].indirect(offs_t[:]))
 
         def bank(b, name):
             return psum.tile([P, S], F32, name=name, tag="bank%d" % b)
@@ -109,7 +118,7 @@ def tile_picked_zgru_gru_po_kernel(
                 lhsT=wq[0][:, cols].bitcast(FP8X4),
                 lhsT_scale=wq[1][:, cols],
                 rhs=aq[0][:].bitcast(FP8X4),
-                rhs_scale=aq[1][:],
+                rhs_scale=aq[1],
                 start=start,
                 stop=stop,
             )
@@ -117,41 +126,37 @@ def tile_picked_zgru_gru_po_kernel(
         xw_tab = load_words(x_words, "xw_tab")
         nc.sync.dma_start(offs_t[:], offs)
         carry0 = load_carry(0, "carry0")
-        load_scales(x_scales, xs_tab)
+        load_scales(x_scales, xs_tab, 0)
         w2_raw = load_weight(w2, "w2_raw", "raw_a")
         nc.sync.dma_start(tok_t[:], tok)
         ew_tab = load_words(e_words, "ew_tab")
-        load_scales(e_scales, es_tab)
+        load_scales(e_scales, es_tab, 4)
         w3_raw = load_weight(w3, "w3_raw", "raw_b")
 
         x_words_g = tl([P, S], U32, "x_words_g")
         x_scales_g = tl([P, S], U8, "x_scales_g")
         nc.vector.tensor_copy(x_words_g[:], xw_tab[:].bitcast(U32).indirect(offs_t[:]))
-        carry1 = load_carry(1, "xw_tab")
-        old = [gather_carry(carry0, tl([P, S], F32, "old0"))]
+        old0 = tl([P, S], F32, "old0")
+        gather_carry(carry0, old0[:])
         nc.vector.tensor_copy(x_scales_g[:], xs_tab[:].indirect(offs_t[:]))
-        xq = (x_words_g, x_scales_g)
-        w2_g = at([P, PACK * N], BF16, "w2_g", 0)
-        cast(w2_raw, w2_g, "v")
+        xq = (x_words_g, x_scales_g[:])
+        w2_q = shared_cast_quant(w2_raw, tl([P, 2 * N], BF16, "w2_lo"), at([P, 2 * N], BF16, "w2_hi", 1024), "w2")
         v3_raw = load_weight(v3, "v3_raw", "raw_a")
-        w2_q = quant(w2_g, "w2")
         r_ps = [bank(t, "r_ps%d" % t) for t in range(PACK)]
         for t in range(PACK):
             mm(r_ps[t], w2_q, xq, t, True, True)
         eq = gather_packed(ew_tab, es_tab, tok_t, at([P, S], U32, "e_words_g", 0), at([P, S], U8, "e_scales_g", 2048))
-        w3_g = at([P, PACK * N], BF16, "w3_g", 2560)
-        cast(w3_raw, w3_g, "v")
-        w1_raw = load_weight(w1, "w1_raw", "raw_b")
+        carry1 = load_carry(1, "ew_tab")
+        w1_raw = load_weight(w1, "w1_raw", "es_tab")
+        w3_q = shared_cast_quant(w3_raw, at([P, 2 * N], BF16, "w3_lo", 2560), tl([P, 2 * N], BF16, "w3_hi", "w2_lo"), "w3")
+        v1_raw = load_weight(v1, "v1_raw", "raw_b")
         tr = [tl([P, S], F32, "tr%d" % t) for t in range(PACK)]
         for t in range(PACK):
             nc.scalar.activation(tr[t][:], r_ps[t][:], TANH, scale=0.5)
-        w3_q = quant(w3_g, "w3")
         d_ps = [bank(4 + t, "d_ps%d" % t) for t in range(PACK)]
         for t in range(PACK):
             mm(d_ps[t], w3_q, xq, t, True, True)
-        old.append(gather_carry(carry1, at([P, S], F32, "old1", 4608)))
-        v1_raw = load_weight(v1, "v1_raw", "xw_tab")
-        v3_g = at([P, PACK * N], BF16, "v3_g", 8192)
+        v3_g = tl([P, PACK * N], BF16, "v3_g")
         cast(v3_raw, v3_g, "s")
         u = [tl([P, S], F32, "u%d" % t) for t in range(PACK)]
         for t in range(PACK):
@@ -162,29 +167,32 @@ def tile_picked_zgru_gru_po_kernel(
         c_ps = [bank(t, "c_ps%d" % t) for t in range(PACK)]
         for t in range(PACK):
             mm(c_ps[t], v3_q, eq, t, True, True)
-        w1_g = at([P, PACK * N], BF16, "w1_g", 12288)
+        old1 = tl([P, S], F32, "old1", "v3_g")
+        gather_carry(carry1, old1[:])
+        w1_g = tl([P, PACK * N], BF16, "w1_g")
         cast(w1_raw, w1_g, "s")
+        v1_g = tl([P, PACK * N], BF16, "v1_g")
+        cast(v1_raw, v1_g, "s")
         v = [tl([P, S], F32, "v%d" % t) for t in range(PACK)]
         for t in range(PACK):
             nc.vector.scalar_tensor_tensor(v[t][:], u[t][:], 0.5, c_ps[t][:], MULT, ADD)
-        w1_q = quant(w1_g, "w1")
+        w1_q = quant(w1_g, "w1", "u3")
         z_ps = [bank(4 + t, "z_ps%d" % t) for t in range(PACK)]
         for t in range(PACK):
             mm(z_ps[t], w1_q, xq, t, True, False)
-        g = tl([P, PACK, S], F32, "g")
-        v1_g = at([P, PACK * N], BF16, "v1_g", 16384)
-        cast(v1_raw, v1_g, "s")
+        g = tl([P, PACK, S], F32, "g", "raw_b")
         for t in range(PACK):
             nc.scalar.activation(g[:, t, :], v[t][:], TANH)
-        v1_q = quant(v1_g, "v1")
+        old23 = tl([P, 2, S], F32, "old23", "w1_g")
+        gather_carry(carry2, old23[:, 0, :])
+        gather_carry(carry3, old23[:, 1, :])
+        v1_q = quant(v1_g, "v1", "tr1")
         for t in range(PACK):
             mm(z_ps[t], v1_q, eq, t, False, True)
-        old.append(gather_carry(carry2, at([P, S], F32, "old2", 16384)))
-        old.append(gather_carry(carry3, at([P, S], F32, "old3", 18432)))
+        olds = [(slice(0, 1), old0[:].unsqueeze(1)), (slice(1, 2), old1[:].unsqueeze(1)), (slice(2, 4), old23[:])]
         d = tl([P, PACK, S], F32, "d")
-        for t in range(PACK):
-            engine = nc.gpsimd if t in [0,1] else nc.vector
-            engine.tensor_tensor(d[:, t, :], g[:, t, :], old[t][:], SUB)
+        for ts, old in olds:
+            nc.vector.tensor_tensor(d[:, ts, :], g[:, ts, :], old, SUB)
 
         y_codes = tl([P, S], U32, "y_codes")
         y_scales = tl([P, S], U8, "y_scales")
@@ -202,8 +210,8 @@ def tile_picked_zgru_gru_po_kernel(
             cols = slice(h * HALF, (h + 1) * HALF)
             for a in range(0, PACK, 2):
                 nc.vector.scalar_tensor_tensor(e[:, a : a + 2, cols], tz[:, a : a + 2, cols], 1.0, d[:, a : a + 2, cols], ADD, MULT)
-            for t in range(PACK):
-                nc.vector.scalar_tensor_tensor(y[:, t, cols], e[:, t, cols], 0.5, old[t][:, cols], MULT, ADD)
+            for ts, old in olds:
+                nc.vector.scalar_tensor_tensor(y[:, ts, cols], e[:, ts, cols], 0.5, old[:, :, cols], MULT, ADD)
             nc.sync.dma_start(out_rows[:, :, cols], y[:, :, cols])
             dst = yb[h][:].rearrange("p (c i) t -> p c t i", i=4)
             src = y[:, :, cols].rearrange("p t (c i) -> p c t i", i=4)

@@ -43,16 +43,6 @@ def tile_picked_zgru_gru_po_kernel(
         def at(shape, dt, name, offset):
             return laid.tile(shape, dt, name=name, align_bytes=64, offset=offset)
 
-        warm_in = tl([P, 1], F32, "warm_in")
-        warm_out = tl([P, 1], F32, "warm_out")
-        nc.vector.memset(warm_in[:], 0.0)
-        nc.scalar.activation(warm_out[:], warm_in[:], TANH)
-
-        xs_tab = tl([P, T], U8, "xs_tab")
-        es_tab = tl([P, T], U8, "es_tab")
-        nc.gpsimd.memset(xs_tab[:].bitcast(I32), 0)
-        nc.vector.memset(es_tab[:].bitcast(I32), 0)
-
         def load_scales(src, tab, row):
             for q in range(4):
                 nc.sync.dma_start(tab[32 * q + row : 32 * q + row + 4, :].bitcast(I32), src[0, 4 * q : 4 * q + 4, :].bitcast(I32))
@@ -62,137 +52,133 @@ def tile_picked_zgru_gru_po_kernel(
             nc.sync.dma_start(tab[:], src[0].rearrange("p n t -> p (n t)").bitcast(I32))
             return tab
 
-        def load_weight(w, name, tag):
-            raw = tl([P, PACK, N], F32, name, tag)
+        def load_weight(w, name):
+            raw = tl([P, PACK, N], F32, name)
             nc.sync.dma_start(raw[:], w.rearrange("(p j) c -> p j c", j=PACK))
             return raw
 
-        def load_carry(t, tag):
-            tab = tl([P, T], F32, "carry%d" % t, tag)
+        def load_carry(t):
+            tab = tl([P, T], F32, "carry%d" % t)
             nc.sync.dma_start(tab[:], carry.rearrange("(p t) c -> p t c", t=PACK)[:, t, :])
             return tab
 
-        def cast(raw, grouped, helper):
-            dst = grouped[:].rearrange("p (t m j) -> p m j t", t=PACK, j=PACK)
-            src = raw[:].rearrange("p j (m t) -> p m j t", t=PACK)
-            if helper == "v":
-                nc.vector.tensor_copy(dst[:, :, :, 0:2], src[:, :, :, 0:2])
-            if helper == "g":
-                nc.gpsimd.tensor_scalar(dst[:, :, :, 0:2], src[:, :, :, 0:2], 1.0, 0.0, MULT, ADD)
-            if helper == "s":
-                nc.scalar.copy(dst, src)
-            else:
-                nc.scalar.copy(dst[:, :, :, 2:PACK], src[:, :, :, 2:PACK])
+        def dealt(raw, t0, t1):
+            return raw[:].rearrange("p j (m t) -> p m j t", t=PACK)[:, :, :, t0:t1]
+
+        def cast(copy, raw, t0, t1, grouped):
+            copy(grouped[:].rearrange("p (t m j) -> p m j t", t=t1 - t0, j=PACK), dealt(raw, t0, t1))
+            return grouped
 
         def quant(grouped, name, tag=None):
-            codes = tl([P, N], U32, name + "_codes", tag)
-            scales = tl([P, N], U8, name + "_scales")
+            width = grouped.shape[1] // PACK
+            codes = tl([P, width], U32, name + "_codes", tag)
+            scales = tl([P, width], U8, name + "_scales")
             nc.vector.quantize_mx(out=codes[:].bitcast(FP8X4), scales=scales[:], in_=grouped[:])
-            return codes, scales
-
-        def shared_cast_quant(raw, lo, hi, name):
-            src = raw[:].rearrange("p j (m t) -> p m j t", t=PACK)
-            nc.vector.tensor_copy(lo[:].rearrange("p (t m j) -> p m j t", t=2, j=PACK), src[:, :, :, 0:2])
-            nc.scalar.copy(hi[:].rearrange("p (t m j) -> p m j t", t=2, j=PACK), src[:, :, :, 2:PACK])
-            codes = tl([P, N], U32, name + "_codes")
-            scales = tl([P, N], U8, name + "_scales")
-            for cols, half in ((slice(0, N // 2), lo), (slice(N // 2, N), hi)):
-                nc.vector.quantize_mx(out=codes[:, cols].bitcast(FP8X4), scales=scales[:, cols], in_=half[:])
-            return codes, scales
-
-        def gather_packed(wtab, stab, lst, words, scales):
-            nc.vector.tensor_copy(words[:], wtab[:].bitcast(U32).indirect(lst[:]))
-            nc.vector.tensor_copy(scales[:], stab[:].indirect(lst[:]))
-            return words, scales[4:P, :]
-
-        def gather_carry(tab, dst):
-            nc.vector.tensor_copy(dst, tab[:].indirect(offs_t[:]))
+            return [(codes[:, c : c + P], scales[:, c : c + P]) for c in range(0, width, P)]
 
         def bank(b, name):
             return psum.tile([P, S], F32, name=name, tag="bank%d" % b)
 
         def mm(acc, wq, aq, t, start, stop):
-            cols = slice(t * P, (t + 1) * P)
             nc.tensor.matmul_mx(
                 out=acc[:],
-                lhsT=wq[0][:, cols].bitcast(FP8X4),
-                lhsT_scale=wq[1][:, cols],
+                lhsT=wq[t][0].bitcast(FP8X4),
+                lhsT_scale=wq[t][1],
                 rhs=aq[0][:].bitcast(FP8X4),
                 rhs_scale=aq[1],
                 start=start,
                 stop=stop,
             )
 
+        xs_tab = tl([P, T], U8, "xs_tab")
+        es_tab = tl([P, T], U8, "es_tab")
+        nc.gpsimd.memset(xs_tab[:].bitcast(I32), 0)
+        nc.vector.memset(es_tab[:].bitcast(I32), 0)
+
+        half_a = at([P, 16], F32, "half_a", 0)
+        half_b = at([P, 16], F32, "half_b", 2048)
+        nc.vector.memset(half_a[:], 0.5)
+        nc.vector.memset(half_b[:], 0.5)
+
         xw_tab = load_words(x_words, "xw_tab")
         nc.sync.dma_start(offs_t[:], offs)
-        carry0 = load_carry(0, "carry0")
         load_scales(x_scales, xs_tab, 0)
-        w2_raw = load_weight(w2, "w2_raw", "raw_a")
         nc.sync.dma_start(tok_t[:], tok)
-        ew_tab = load_words(e_words, "ew_tab")
+        w2_raw = load_weight(w2, "w2_raw")
         load_scales(e_scales, es_tab, 4)
-        w3_raw = load_weight(w3, "w3_raw", "raw_b")
+        w3_raw = at([P, PACK, N], F32, "w3_raw", 4096)
+        nc.sync.dma_start(w3_raw[:], w3.rearrange("(p j) c -> p j c", j=PACK))
+        ew_tab = load_words(e_words, "ew_tab")
+        v3_raw = load_weight(v3, "v3_raw")
+        w1_raw = load_weight(w1, "w1_raw")
+        v1_raw = load_weight(v1, "v1_raw")
+        carries = [load_carry(t) for t in range(PACK)]
 
         x_words_g = tl([P, S], U32, "x_words_g")
         x_scales_g = tl([P, S], U8, "x_scales_g")
         nc.vector.tensor_copy(x_words_g[:], xw_tab[:].bitcast(U32).indirect(offs_t[:]))
-        old0 = tl([P, S], F32, "old0")
-        gather_carry(carry0, old0[:])
         nc.vector.tensor_copy(x_scales_g[:], xs_tab[:].indirect(offs_t[:]))
         xq = (x_words_g, x_scales_g[:])
-        w2_q = shared_cast_quant(w2_raw, tl([P, 2 * N], BF16, "w2_lo"), at([P, 2 * N], BF16, "w2_hi", 1024), "w2")
-        v3_raw = load_weight(v3, "v3_raw", "raw_a")
+        w2_lo = cast(nc.vector.tensor_copy, w2_raw, 0, 2, tl([P, 2 * N], BF16, "w2_lo"))
+        w2_hi = cast(nc.scalar.copy, w2_raw, 2, 4, tl([P, 2 * N], BF16, "w2_hi"))
+        w2_q = quant(w2_lo, "w2_lo") + quant(w2_hi, "w2_hi")
+        e_scales_g = tl([P, S], U8, "e_scales_g", "xs_tab")
+        nc.vector.tensor_copy(e_scales_g[:], es_tab[:].indirect(tok_t[:]))
         r_ps = [bank(t, "r_ps%d" % t) for t in range(PACK)]
         for t in range(PACK):
             mm(r_ps[t], w2_q, xq, t, True, True)
-        eq = gather_packed(ew_tab, es_tab, tok_t, at([P, S], U32, "e_words_g", 0), at([P, S], U8, "e_scales_g", 2048))
-        carry1 = load_carry(1, "ew_tab")
-        w1_raw = load_weight(w1, "w1_raw", "es_tab")
-        w3_q = shared_cast_quant(w3_raw, at([P, 2 * N], BF16, "w3_lo", 2560), tl([P, 2 * N], BF16, "w3_hi", "w2_lo"), "w3")
-        v1_raw = load_weight(v1, "v1_raw", "raw_b")
-        tr = [tl([P, S], F32, "tr%d" % t) for t in range(PACK)]
-        for t in range(PACK):
-            nc.scalar.activation(tr[t][:], r_ps[t][:], TANH, scale=0.5)
+        w3_lo = cast(nc.vector.tensor_copy, w3_raw, 0, 2, tl([P, 2 * N], BF16, "w3_lo"))
+        w3_hi = cast(nc.scalar.copy, w3_raw, 2, 4, tl([P, 2 * N], BF16, "w3_hi", "w2_lo"))
+        w3_q = quant(w3_lo, "w3_lo") + quant(w3_hi, "w3_hi")
         d_ps = [bank(4 + t, "d_ps%d" % t) for t in range(PACK)]
         for t in range(PACK):
             mm(d_ps[t], w3_q, xq, t, True, True)
-        v3_g = tl([P, PACK * N], BF16, "v3_g")
-        cast(v3_raw, v3_g, "s")
-        u = [tl([P, S], F32, "u%d" % t) for t in range(PACK)]
+        tr = [tl([P, S], F32, "tr0")] + [at([P, S], F32, "tr%d" % t, 4096 + 2048 * t) for t in range(1, PACK)]
         for t in range(PACK):
+            half = half_a if t < 3 else half_b
+            nc.scalar.activation(tr[t][:], r_ps[t][:], TANH, scale=half[:, 0:1])
+        e_words_g = tl([P, S], U32, "e_words_g", "w3_lo")
+        nc.vector.tensor_copy(e_words_g[:], ew_tab[:].bitcast(U32).indirect(tok_t[:]))
+        eq = (e_words_g, e_scales_g[4:P, :])
+        u = [tl([P, S], F32, "u%d" % t) for t in range(PACK)]
+
+        def reset(t):
             nc.vector.scalar_tensor_tensor(u[t][:], tr[t][:], 1.0, d_ps[t][:], ADD, MULT)
-        carry2 = load_carry(2, "tr0")
-        carry3 = load_carry(3, "tr1")
-        v3_q = quant(v3_g, "v3")
+
+        v3_lo = cast(nc.scalar.copy, v3_raw, 0, 2, at([P, 2 * N], BF16, "v3_lo", 0))
+        v3_hi = cast(nc.scalar.copy, v3_raw, 2, 4, at([P, 2 * N], BF16, "v3_hi", 2048))
+        for t in range(3):
+            reset(t)
+        v3_q = quant(v3_lo, "v3_lo")
+        reset(3)
+        v3_q = v3_q + quant(v3_hi, "v3_hi")
         c_ps = [bank(t, "c_ps%d" % t) for t in range(PACK)]
         for t in range(PACK):
             mm(c_ps[t], v3_q, eq, t, True, True)
-        old1 = tl([P, S], F32, "old1", "v3_g")
-        gather_carry(carry1, old1[:])
-        w1_g = tl([P, PACK * N], BF16, "w1_g")
-        cast(w1_raw, w1_g, "s")
-        v1_g = tl([P, PACK * N], BF16, "v1_g")
-        cast(v1_raw, v1_g, "s")
+        w1_g = cast(nc.scalar.copy, w1_raw, 0, 4, tl([P, PACK * N], BF16, "w1_g", "tr0"))
         v = [tl([P, S], F32, "v%d" % t) for t in range(PACK)]
         for t in range(PACK):
             nc.vector.scalar_tensor_tensor(v[t][:], u[t][:], 0.5, c_ps[t][:], MULT, ADD)
-        w1_q = quant(w1_g, "w1", "u3")
+        w1_q = quant(w1_g, "w1", "u2")
         z_ps = [bank(4 + t, "z_ps%d" % t) for t in range(PACK)]
         for t in range(PACK):
             mm(z_ps[t], w1_q, xq, t, True, False)
-        g = tl([P, PACK, S], F32, "g", "raw_b")
+        g = tl([P, PACK, S], F32, "g")
         for t in range(PACK):
             nc.scalar.activation(g[:, t, :], v[t][:], TANH)
-        old23 = tl([P, 2, S], F32, "old23", "w1_g")
-        gather_carry(carry2, old23[:, 0, :])
-        gather_carry(carry3, old23[:, 1, :])
-        v1_q = quant(v1_g, "v1", "tr1")
+        v1_lo = cast(nc.scalar.copy, v1_raw, 0, 2, tl([P, 2 * N], BF16, "v1_lo", "v2"))
+        v1_hi = cast(nc.scalar.copy, v1_raw, 2, 4, tl([P, 2 * N], BF16, "v1_hi", "v3"))
+        d = [tl([P, S], F32, "d%d" % t, "v2" if t == 3 else None) for t in range(PACK)]
+
+        def differ(t):
+            nc.vector.tensor_tensor(d[t][:], carries[t][:].indirect(offs_t[:]), g[:, t, :], SUB)
+
+        for t in range(3):
+            differ(t)
+        v1_q = quant(v1_lo, "v1_lo") + quant(v1_hi, "v1_hi")
+        differ(3)
         for t in range(PACK):
             mm(z_ps[t], v1_q, eq, t, False, True)
-        olds = [(slice(0, 1), old0[:].unsqueeze(1)), (slice(1, 2), old1[:].unsqueeze(1)), (slice(2, 4), old23[:])]
-        d = tl([P, PACK, S], F32, "d")
-        for ts, old in olds:
-            nc.vector.tensor_tensor(d[:, ts, :], g[:, ts, :], old, SUB)
 
         y_codes = tl([P, S], U32, "y_codes")
         y_scales = tl([P, S], U8, "y_scales")
@@ -201,30 +187,47 @@ def tile_picked_zgru_gru_po_kernel(
         tz = tl([P, PACK, S], F32, "tz")
         e = tl([P, PACK, S], F32, "e")
         y = tl([P, PACK, S], F32, "y")
-        yb = [tl([P, HALF, PACK], BF16, "yb%d" % h) for h in range(2)]
-        for h in range(2):
-            cols = slice(h * HALF, (h + 1) * HALF)
-            for t in range(PACK):
-                nc.scalar.activation(tz[:, t, cols], z_ps[t][:, cols], TANH, scale=0.5)
-        for h in range(2):
-            cols = slice(h * HALF, (h + 1) * HALF)
-            for a in range(0, PACK, 2):
-                nc.vector.scalar_tensor_tensor(e[:, a : a + 2, cols], tz[:, a : a + 2, cols], 1.0, d[:, a : a + 2, cols], ADD, MULT)
-            for ts, old in olds:
-                nc.vector.scalar_tensor_tensor(y[:, ts, cols], e[:, ts, cols], 0.5, old[:, :, cols], MULT, ADD)
-            nc.sync.dma_start(out_rows[:, :, cols], y[:, :, cols])
-            dst = yb[h][:].rearrange("p (c i) t -> p c t i", i=4)
-            src = y[:, :, cols].rearrange("p t (c i) -> p c t i", i=4)
-            vec = 0 if h == 0 else 40
-            if vec > 0:
-                nc.vector.tensor_copy(dst[:, 0:vec], src[:, 0:vec])
-            nc.scalar.copy(dst[:, vec:], src[:, vec:])
-        for h in range(2):
-            cols = slice(h * HALF, (h + 1) * HALF)
+        for t in range(PACK):
+            nc.scalar.activation(tz[:, t, :], z_ps[t][:], TANH, scale=-0.5)
+
+        def step(t, cols):
+            nc.vector.scalar_tensor_tensor(e[:, t, cols], tz[:, t, cols], 1.0, d[t][:, cols], ADD, MULT)
+
+        def blend(t, cols):
+            nc.vector.scalar_tensor_tensor(y[:, t, cols], e[:, t, cols], 0.5, g[:, t, cols], MULT, ADD)
+
+        def store(ts, cols):
+            nc.sync.dma_start(out_rows[:, ts, cols], y[:, ts, cols])
+
+        def regroup(copy, grouped, c0, c1, first):
+            dst = grouped[:, c0 - first : c1 - first, :].rearrange("p (c i) t -> p c t i", i=4)
+            copy(dst, y[:, :, c0:c1].rearrange("p t (c i) -> p c t i", i=4))
+
+        def planes(grouped, cols):
             nc.vector.quantize_mx(
-                out=y_codes[:, cols].bitcast(FP8X4), scales=y_scales[:, cols], in_=yb[h][:].rearrange("p c t -> p (c t)")
+                out=y_codes[:, cols].bitcast(FP8X4), scales=y_scales[:, cols], in_=grouped[:].rearrange("p c t -> p (c t)")
             )
             nc.sync.dma_start(out_words[:, cols], y_codes[:, cols].bitcast(I32))
+
+        whole, left, right = slice(0, S), slice(0, HALF), slice(HALF, S)
+        step(0, whole)
+        step(1, whole)
+        blend(0, whole)
+        blend(1, whole)
+        store(slice(0, 2), whole)
+        yb = [tl([P, HALF, PACK], BF16, "yb%d" % h) for h in range(2)]
+        for cols in (left, right):
+            step(2, cols)
+            step(3, cols)
+            blend(2, cols)
+            blend(3, cols)
+            store(slice(2, 4), cols)
+            if cols is left:
+                regroup(nc.scalar.copy, yb[0], 0, HALF, 0)
+        planes(yb[0], left)
+        regroup(nc.vector.tensor_copy, yb[1], HALF, HALF + 128, HALF)
+        regroup(nc.scalar.copy, yb[1], HALF + 128, S, HALF)
+        planes(yb[1], right)
         for q in range(4):
             queue = nc.scalar if q % 2 else nc.sync
             queue.dma_start(out_2[0, 4 * q : 4 * q + 4, :].bitcast(I32), y_scales[32 * q : 32 * q + 4, :].bitcast(I32))

@@ -22,6 +22,10 @@ S = 512
 T = 1024
 N = 512
 HALF = S // 2
+QUARTER = S // 4
+E_PLANE = 4
+TILE_BYTES = 2048
+W3_AT = 2 * TILE_BYTES
 
 
 def tile_picked_zgru_gru_po_kernel(
@@ -37,197 +41,194 @@ def tile_picked_zgru_gru_po_kernel(
         offs_t = lists.tile([P, S // 16], U16, name="offs_t")
         tok_t = lists.tile([P, S // 16], U16, name="tok_t")
 
-        def tl(shape, dt, name, tag=None):
-            return sb.tile(shape, dt, name=name, tag=tag or name, align_bytes=64)
+        def tagged(shape, dt, name, over=None):
+            return sb.tile(shape, dt, name=name, tag=over or name, align_bytes=64)
 
-        def at(shape, dt, name, offset):
+        def placed(shape, dt, name, offset):
             return laid.tile(shape, dt, name=name, align_bytes=64, offset=offset)
 
-        def load_scales(src, tab, row):
+        def load_scales(src, tab, first_row):
             for q in range(4):
-                nc.sync.dma_start(tab[32 * q + row : 32 * q + row + 4, :].bitcast(I32), src[0, 4 * q : 4 * q + 4, :].bitcast(I32))
+                rows = slice(32 * q + first_row, 32 * q + first_row + 4)
+                nc.sync.dma_start(tab[rows, :].bitcast(I32), src[0, 4 * q : 4 * q + 4, :].bitcast(I32))
 
         def load_words(src, name):
-            tab = tl([P, T], I32, name)
+            tab = tagged([P, T], I32, name)
             nc.sync.dma_start(tab[:], src[0].rearrange("p n t -> p (n t)").bitcast(I32))
             return tab
 
-        def load_weight(w, name):
-            raw = tl([P, PACK, N], F32, name)
+        def load_weight(w, raw):
             nc.sync.dma_start(raw[:], w.rearrange("(p j) c -> p j c", j=PACK))
             return raw
 
         def load_carry(t):
-            tab = tl([P, T], F32, "carry%d" % t)
+            tab = tagged([P, T], F32, "carry%d" % t)
             nc.sync.dma_start(tab[:], carry.rearrange("(p t) c -> p t c", t=PACK)[:, t, :])
             return tab
 
-        def dealt(raw, t0, t1):
-            return raw[:].rearrange("p j (m t) -> p m j t", t=PACK)[:, :, :, t0:t1]
-
-        def cast(copy, raw, t0, t1, grouped):
-            copy(grouped[:].rearrange("p (t m j) -> p m j t", t=t1 - t0, j=PACK), dealt(raw, t0, t1))
+        def round_weight(copy, raw, t0, t1, grouped):
+            src = raw[:].rearrange("p j (m t) -> p m j t", t=PACK)[:, :, :, t0:t1]
+            copy(grouped[:].rearrange("p (t m j) -> p m j t", t=t1 - t0, j=PACK), src)
             return grouped
 
-        def quant(grouped, name, tag=None):
+        def quantise(grouped, name, over=None):
             width = grouped.shape[1] // PACK
-            codes = tl([P, width], U32, name + "_codes", tag)
-            scales = tl([P, width], U8, name + "_scales")
+            codes = tagged([P, width], U32, name + "_codes", over)
+            scales = tagged([P, width], U8, name + "_scales")
             nc.vector.quantize_mx(out=codes[:].bitcast(FP8X4), scales=scales[:], in_=grouped[:])
             return [(codes[:, c : c + P], scales[:, c : c + P]) for c in range(0, width, P)]
 
-        def bank(b, name):
-            return psum.tile([P, S], F32, name=name, tag="bank%d" % b)
+        def banks(first, name):
+            return [psum.tile([P, S], F32, name="%s%d" % (name, t), tag="bank%d" % (first + t)) for t in range(PACK)]
 
-        def mm(acc, wq, aq, t, start, stop):
-            nc.tensor.matmul_mx(
-                out=acc[:],
-                lhsT=wq[t][0].bitcast(FP8X4),
-                lhsT_scale=wq[t][1],
-                rhs=aq[0][:].bitcast(FP8X4),
-                rhs_scale=aq[1],
-                start=start,
-                stop=stop,
-            )
+        def product(acc, weight, picked, start, stop):
+            for t in range(PACK):
+                nc.tensor.matmul_mx(
+                    out=acc[t][:],
+                    lhsT=weight[t][0].bitcast(FP8X4),
+                    lhsT_scale=weight[t][1],
+                    rhs=picked[0].bitcast(FP8X4),
+                    rhs_scale=picked[1],
+                    start=start,
+                    stop=stop,
+                )
 
-        xs_tab = tl([P, T], U8, "xs_tab")
-        es_tab = tl([P, T], U8, "es_tab")
+        xs_tab = tagged([P, T], U8, "xs_tab")
+        es_tab = tagged([P, T], U8, "es_tab")
         nc.gpsimd.memset(xs_tab[:].bitcast(I32), 0)
         nc.vector.memset(es_tab[:].bitcast(I32), 0)
 
-        half_a = at([P, 16], F32, "half_a", 0)
-        half_b = at([P, 16], F32, "half_b", 2048)
-        nc.vector.memset(half_a[:], 0.5)
-        nc.vector.memset(half_b[:], 0.5)
+        half_lo = placed([P, 1], F32, "half_lo", 0)
+        half_hi = placed([P, 1], F32, "half_hi", TILE_BYTES)
+        nc.vector.memset(half_lo[:], 0.5)
+        nc.vector.memset(half_hi[:], 0.5)
 
         xw_tab = load_words(x_words, "xw_tab")
         nc.sync.dma_start(offs_t[:], offs)
         load_scales(x_scales, xs_tab, 0)
         nc.sync.dma_start(tok_t[:], tok)
-        w2_raw = load_weight(w2, "w2_raw")
-        load_scales(e_scales, es_tab, 4)
-        w3_raw = at([P, PACK, N], F32, "w3_raw", 4096)
-        nc.sync.dma_start(w3_raw[:], w3.rearrange("(p j) c -> p j c", j=PACK))
+        w2_raw = load_weight(w2, tagged([P, PACK, N], F32, "w2_raw"))
+        load_scales(e_scales, es_tab, E_PLANE)
+        w3_raw = load_weight(w3, placed([P, PACK, N], F32, "w3_raw", W3_AT))
         ew_tab = load_words(e_words, "ew_tab")
-        v3_raw = load_weight(v3, "v3_raw")
-        w1_raw = load_weight(w1, "w1_raw")
-        v1_raw = load_weight(v1, "v1_raw")
+        v3_raw = load_weight(v3, tagged([P, PACK, N], F32, "v3_raw"))
+        w1_raw = load_weight(w1, tagged([P, PACK, N], F32, "w1_raw"))
+        v1_raw = load_weight(v1, tagged([P, PACK, N], F32, "v1_raw"))
         carries = [load_carry(t) for t in range(PACK)]
 
-        x_words_g = tl([P, S], U32, "x_words_g")
-        x_scales_g = tl([P, S], U8, "x_scales_g")
+        x_words_g = tagged([P, S], U32, "x_words_g")
+        x_scales_g = tagged([P, S], U8, "x_scales_g")
         nc.vector.tensor_copy(x_words_g[:], xw_tab[:].bitcast(U32).indirect(offs_t[:]))
         nc.vector.tensor_copy(x_scales_g[:], xs_tab[:].indirect(offs_t[:]))
-        xq = (x_words_g, x_scales_g[:])
-        w2_lo = cast(nc.vector.tensor_copy, w2_raw, 0, 2, tl([P, 2 * N], BF16, "w2_lo"))
-        w2_hi = cast(nc.scalar.copy, w2_raw, 2, 4, tl([P, 2 * N], BF16, "w2_hi"))
-        w2_q = quant(w2_lo, "w2_lo") + quant(w2_hi, "w2_hi")
-        e_scales_g = tl([P, S], U8, "e_scales_g", "xs_tab")
+        x_picked = (x_words_g[:], x_scales_g[:])
+        w2_lo = round_weight(nc.vector.tensor_copy, w2_raw, 0, 2, tagged([P, 2 * N], BF16, "w2_lo"))
+        w2_hi = round_weight(nc.scalar.copy, w2_raw, 2, 4, tagged([P, 2 * N], BF16, "w2_hi"))
+        w2_q = quantise(w2_lo, "w2_lo") + quantise(w2_hi, "w2_hi")
+        e_scales_g = tagged([P, S], U8, "e_scales_g", "xs_tab")
         nc.vector.tensor_copy(e_scales_g[:], es_tab[:].indirect(tok_t[:]))
-        r_ps = [bank(t, "r_ps%d" % t) for t in range(PACK)]
+        r_ps = banks(0, "r_ps")
+        product(r_ps, w2_q, x_picked, True, True)
+
+        w3_lo = round_weight(nc.vector.tensor_copy, w3_raw, 0, 2, tagged([P, 2 * N], BF16, "w3_lo"))
+        w3_hi = round_weight(nc.scalar.copy, w3_raw, 2, 4, tagged([P, 2 * N], BF16, "w3_hi", "w2_lo"))
+        w3_q = quantise(w3_lo, "w3_lo") + quantise(w3_hi, "w3_hi")
+        wx_ps = banks(PACK, "wx_ps")
+        product(wx_ps, w3_q, x_picked, True, True)
+
+        tanh_r = [tagged([P, S], F32, "tanh_r0")]
+        tanh_r.extend(placed([P, S], F32, "tanh_r%d" % t, W3_AT + TILE_BYTES * t) for t in range(1, PACK))
         for t in range(PACK):
-            mm(r_ps[t], w2_q, xq, t, True, True)
-        w3_lo = cast(nc.vector.tensor_copy, w3_raw, 0, 2, tl([P, 2 * N], BF16, "w3_lo"))
-        w3_hi = cast(nc.scalar.copy, w3_raw, 2, 4, tl([P, 2 * N], BF16, "w3_hi", "w2_lo"))
-        w3_q = quant(w3_lo, "w3_lo") + quant(w3_hi, "w3_hi")
-        d_ps = [bank(4 + t, "d_ps%d" % t) for t in range(PACK)]
-        for t in range(PACK):
-            mm(d_ps[t], w3_q, xq, t, True, True)
-        tr = [tl([P, S], F32, "tr0")] + [at([P, S], F32, "tr%d" % t, 4096 + 2048 * t) for t in range(1, PACK)]
-        for t in range(PACK):
-            half = half_a if t < 3 else half_b
-            nc.scalar.activation(tr[t][:], r_ps[t][:], TANH, scale=half[:, 0:1])
-        e_words_g = tl([P, S], U32, "e_words_g", "w3_lo")
+            half = half_lo if t < PACK - 1 else half_hi
+            nc.scalar.activation(tanh_r[t][:], r_ps[t][:], TANH, scale=half[:])
+        e_words_g = tagged([P, S], U32, "e_words_g", "w3_lo")
         nc.vector.tensor_copy(e_words_g[:], ew_tab[:].bitcast(U32).indirect(tok_t[:]))
-        eq = (e_words_g, e_scales_g[4:P, :])
-        u = [tl([P, S], F32, "u%d" % t) for t in range(PACK)]
+        e_picked = (e_words_g[:], e_scales_g[E_PLANE:P, :])
+
+        twice_rwx = [tagged([P, S], F32, "twice_rwx%d" % t) for t in range(PACK)]
 
         def reset(t):
-            nc.vector.scalar_tensor_tensor(u[t][:], tr[t][:], 1.0, d_ps[t][:], ADD, MULT)
+            nc.vector.scalar_tensor_tensor(twice_rwx[t][:], tanh_r[t][:], 1.0, wx_ps[t][:], ADD, MULT)
 
-        v3_lo = cast(nc.scalar.copy, v3_raw, 0, 2, at([P, 2 * N], BF16, "v3_lo", 0))
-        v3_hi = cast(nc.scalar.copy, v3_raw, 2, 4, at([P, 2 * N], BF16, "v3_hi", 2048))
-        for t in range(3):
+        v3_lo = round_weight(nc.scalar.copy, v3_raw, 0, 2, placed([P, 2 * N], BF16, "v3_lo", 0))
+        v3_hi = round_weight(nc.scalar.copy, v3_raw, 2, 4, placed([P, 2 * N], BF16, "v3_hi", TILE_BYTES))
+        for t in range(PACK - 1):
             reset(t)
-        v3_q = quant(v3_lo, "v3_lo")
-        reset(3)
-        v3_q = v3_q + quant(v3_hi, "v3_hi")
-        c_ps = [bank(t, "c_ps%d" % t) for t in range(PACK)]
+        v3_q = quantise(v3_lo, "v3_lo")
+        reset(PACK - 1)
+        v3_q = v3_q + quantise(v3_hi, "v3_hi")
+        ve_ps = banks(0, "ve_ps")
+        product(ve_ps, v3_q, e_picked, True, True)
+
+        w1_g = round_weight(nc.scalar.copy, w1_raw, 0, 4, tagged([P, PACK * N], BF16, "w1_g", "tanh_r0"))
+        g_arg = [tagged([P, S], F32, "g_arg%d" % t) for t in range(PACK)]
         for t in range(PACK):
-            mm(c_ps[t], v3_q, eq, t, True, True)
-        w1_g = cast(nc.scalar.copy, w1_raw, 0, 4, tl([P, PACK * N], BF16, "w1_g", "tr0"))
-        v = [tl([P, S], F32, "v%d" % t) for t in range(PACK)]
+            nc.vector.scalar_tensor_tensor(g_arg[t][:], twice_rwx[t][:], 0.5, ve_ps[t][:], MULT, ADD)
+        w1_q = quantise(w1_g, "w1", "twice_rwx2")
+        z_ps = banks(PACK, "z_ps")
+        product(z_ps, w1_q, x_picked, True, False)
+        g = tagged([P, PACK, S], F32, "g")
         for t in range(PACK):
-            nc.vector.scalar_tensor_tensor(v[t][:], u[t][:], 0.5, c_ps[t][:], MULT, ADD)
-        w1_q = quant(w1_g, "w1", "u2")
-        z_ps = [bank(4 + t, "z_ps%d" % t) for t in range(PACK)]
-        for t in range(PACK):
-            mm(z_ps[t], w1_q, xq, t, True, False)
-        g = tl([P, PACK, S], F32, "g")
-        for t in range(PACK):
-            nc.scalar.activation(g[:, t, :], v[t][:], TANH)
-        v1_lo = cast(nc.scalar.copy, v1_raw, 0, 2, tl([P, 2 * N], BF16, "v1_lo", "v2"))
-        v1_hi = cast(nc.scalar.copy, v1_raw, 2, 4, tl([P, 2 * N], BF16, "v1_hi", "v3"))
-        d = [tl([P, S], F32, "d%d" % t, "v2" if t == 3 else None) for t in range(PACK)]
+            nc.scalar.activation(g[:, t, :], g_arg[t][:], TANH)
+
+        v1_lo = round_weight(nc.scalar.copy, v1_raw, 0, 2, tagged([P, 2 * N], BF16, "v1_lo", "g_arg2"))
+        v1_hi = round_weight(nc.scalar.copy, v1_raw, 2, 4, tagged([P, 2 * N], BF16, "v1_hi", "g_arg3"))
+        diff = [tagged([P, S], F32, "diff%d" % t, "g_arg2" if t == PACK - 1 else None) for t in range(PACK)]
 
         def differ(t):
-            nc.vector.tensor_tensor(d[t][:], carries[t][:].indirect(offs_t[:]), g[:, t, :], SUB)
+            nc.vector.tensor_tensor(diff[t][:], carries[t][:].indirect(offs_t[:]), g[:, t, :], SUB)
 
-        for t in range(3):
+        for t in range(PACK - 1):
             differ(t)
-        v1_q = quant(v1_lo, "v1_lo") + quant(v1_hi, "v1_hi")
-        differ(3)
-        for t in range(PACK):
-            mm(z_ps[t], v1_q, eq, t, False, True)
+        v1_q = quantise(v1_lo, "v1_lo") + quantise(v1_hi, "v1_hi")
+        differ(PACK - 1)
+        product(z_ps, v1_q, e_picked, False, True)
 
-        y_codes = tl([P, S], U32, "y_codes")
-        y_scales = tl([P, S], U8, "y_scales")
+        y_codes = tagged([P, S], U32, "y_codes")
+        y_scales = tagged([P, S], U8, "y_scales")
         out_rows = out_0.rearrange("(p t) c -> p t c", t=PACK)
         out_words = out_1[0].rearrange("p n t -> p (n t)").bitcast(I32)
-        tz = tl([P, PACK, S], F32, "tz")
-        e = tl([P, PACK, S], F32, "e")
-        y = tl([P, PACK, S], F32, "y")
+        tanh_keep = tagged([P, PACK, S], F32, "tanh_keep")
+        twice_step = tagged([P, PACK, S], F32, "twice_step")
+        y = tagged([P, PACK, S], F32, "y")
         for t in range(PACK):
-            nc.scalar.activation(tz[:, t, :], z_ps[t][:], TANH, scale=-0.5)
+            nc.scalar.activation(tanh_keep[:, t, :], z_ps[t][:], TANH, scale=-0.5)
 
-        def step(t, cols):
-            nc.vector.scalar_tensor_tensor(e[:, t, cols], tz[:, t, cols], 1.0, d[t][:, cols], ADD, MULT)
+        def blend(tiles, cols):
+            for t in tiles:
+                nc.vector.scalar_tensor_tensor(
+                    twice_step[:, t, cols], tanh_keep[:, t, cols], 1.0, diff[t][:, cols], ADD, MULT
+                )
+            for t in tiles:
+                nc.vector.scalar_tensor_tensor(y[:, t, cols], twice_step[:, t, cols], 0.5, g[:, t, cols], MULT, ADD)
+            rows = slice(tiles.start, tiles.stop)
+            nc.sync.dma_start(out_rows[:, rows, cols], y[:, rows, cols])
 
-        def blend(t, cols):
-            nc.vector.scalar_tensor_tensor(y[:, t, cols], e[:, t, cols], 0.5, g[:, t, cols], MULT, ADD)
+        def round_result(copy, cols, name):
+            grouped = tagged([P, cols.stop - cols.start, PACK], BF16, name)
+            copy(
+                grouped[:].rearrange("p (c i) t -> p c t i", i=4),
+                y[:, :, cols].rearrange("p t (c i) -> p c t i", i=4),
+            )
+            return grouped
 
-        def store(ts, cols):
-            nc.sync.dma_start(out_rows[:, ts, cols], y[:, ts, cols])
-
-        def regroup(copy, grouped, c0, c1, first):
-            dst = grouped[:, c0 - first : c1 - first, :].rearrange("p (c i) t -> p c t i", i=4)
-            copy(dst, y[:, :, c0:c1].rearrange("p t (c i) -> p c t i", i=4))
-
-        def planes(grouped, cols):
+        def quantise_result(grouped, cols):
             nc.vector.quantize_mx(
                 out=y_codes[:, cols].bitcast(FP8X4), scales=y_scales[:, cols], in_=grouped[:].rearrange("p c t -> p (c t)")
             )
-            nc.sync.dma_start(out_words[:, cols], y_codes[:, cols].bitcast(I32))
 
-        whole, left, right = slice(0, S), slice(0, HALF), slice(HALF, S)
-        step(0, whole)
-        step(1, whole)
-        blend(0, whole)
-        blend(1, whole)
-        store(slice(0, 2), whole)
-        yb = [tl([P, HALF, PACK], BF16, "yb%d" % h) for h in range(2)]
-        for cols in (left, right):
-            step(2, cols)
-            step(3, cols)
-            blend(2, cols)
-            blend(3, cols)
-            store(slice(2, 4), cols)
-            if cols is left:
-                regroup(nc.scalar.copy, yb[0], 0, HALF, 0)
-        planes(yb[0], left)
-        regroup(nc.vector.tensor_copy, yb[1], HALF, HALF + 128, HALF)
-        regroup(nc.scalar.copy, yb[1], HALF + 128, S, HALF)
-        planes(yb[1], right)
+        left, right = slice(0, HALF), slice(HALF, S)
+        third, fourth = slice(HALF, HALF + QUARTER), slice(HALF + QUARTER, S)
+        blend(range(0, 2), slice(0, S))
+        blend(range(2, PACK), left)
+        y_left = round_result(nc.scalar.copy, left, "y_left")
+        blend(range(2, PACK), right)
+        quantise_result(y_left, left)
+        nc.sync.dma_start(out_words[:, left], y_codes[:, left].bitcast(I32))
+        y_third = round_result(nc.vector.tensor_copy, third, "y_third")
+        y_fourth = round_result(nc.scalar.copy, fourth, "y_fourth")
+        quantise_result(y_third, third)
+        quantise_result(y_fourth, fourth)
+        nc.sync.dma_start(out_words[:, right], y_codes[:, right].bitcast(I32))
         for q in range(4):
             queue = nc.scalar if q % 2 else nc.sync
             queue.dma_start(out_2[0, 4 * q : 4 * q + 4, :].bitcast(I32), y_scales[32 * q : 32 * q + 4, :].bitcast(I32))

@@ -144,7 +144,8 @@ def tile_picked_zgru_gru_po_kernel(
         nc.vector.tensor_copy(e_words_g[:], ew_tab[:].bitcast(U32).indirect(tok_t[:]))
         e_picked = (e_words_g[:], e_scales_g[E_PLANE:P, :])
 
-        twice_rwx = [tagged([P, S], F32, "twice_rwx%d" % t) for t in range(PACK)]
+        twice_rwx = [tagged([P, S], F32, "twice_rwx%d" % t) for t in range(PACK - 1)]
+        twice_rwx.append(placed([P, S], F32, "twice_rwx3", 0))
 
         def reset(t):
             nc.vector.scalar_tensor_tensor(twice_rwx[t][:], tanh_r[t][:], 1.0, wx_ps[t][:], ADD, MULT)

@@ -1,6 +1,7 @@
 from contextlib import ExitStack
 
 import concourse.mybir as mybir
+from concourse.masks import make_identity
 
 FLOPS = 5 * 2 * 512 * 512 * 512
 
@@ -15,6 +16,7 @@ ADD = mybir.AluOpType.add
 SUB = mybir.AluOpType.subtract
 MULT = mybir.AluOpType.mult
 TANH = mybir.ActivationFunctionType.Tanh
+COPY = mybir.ActivationFunctionType.Copy
 
 P = 128
 PACK = 4
@@ -25,6 +27,7 @@ HALF = S // 2
 QUARTER = S // 4
 E_PLANE = 4
 TILE_BYTES = 2048
+VE_AT = 8 * TILE_BYTES
 W3_AT = 2 * TILE_BYTES
 
 
@@ -76,7 +79,10 @@ def tile_picked_zgru_gru_po_kernel(
             codes = tagged([P, width], U32, name + "_codes", over)
             scales = tagged([P, width], U8, name + "_scales")
             nc.vector.quantize_mx(out=codes[:].bitcast(FP8X4), scales=scales[:], in_=grouped[:])
-            return [(codes[:, c : c + P], scales[:, c : c + P]) for c in range(0, width, P)]
+            return codes, scales
+
+        def by_tile(halves):
+            return [(codes[:, c : c + P], scales[:, c : c + P]) for codes, scales in halves for c in range(0, codes.shape[1], P)]
 
         def banks(first, name):
             return [psum.tile([P, S], F32, name="%s%d" % (name, t), tag="bank%d" % (first + t)) for t in range(PACK)]
@@ -93,15 +99,51 @@ def tile_picked_zgru_gru_po_kernel(
                     stop=stop,
                 )
 
+        def mx_pass(out, stationary, moving):
+            nc.tensor.matmul_mx(
+                out=out,
+                lhsT=stationary[0].bitcast(FP8X4),
+                lhsT_scale=stationary[1],
+                rhs=moving[0].bitcast(FP8X4),
+                rhs_scale=moving[1],
+                start=True,
+                stop=True,
+            )
+
+        def half_product(acc, h, half, picked):
+            for t, tile in enumerate(by_tile([half]), 2 * h):
+                if t:
+                    mx_pass(acc[t][:], tile, picked)
+                    continue
+                for u in range(PACK):
+                    cols = slice(P * u, P * (u + 1))
+                    mx_pass(acc[0][:, cols], (picked[0][:, cols], picked[1][:, cols]), tile)
+
+        def turn_back(acc, src, first):
+            for u in range(PACK):
+                cols = slice(P * u, P * (u + 1))
+                nc.tensor.matmul(
+                    acc[:, cols],
+                    lhsT=src[:, cols],
+                    rhs=ident[:],
+                    is_transpose=True,
+                    start=first and u == 0,
+                    stop=not first and u == PACK - 1,
+                )
+
         xs_tab = tagged([P, T], U8, "xs_tab")
         es_tab = tagged([P, T], U8, "es_tab")
         nc.gpsimd.memset(xs_tab[:].bitcast(I32), 0)
         nc.vector.memset(es_tab[:].bitcast(I32), 0)
+        ident = tagged([P, P], F32, "ident")
+        make_identity(nc, ident[:])
 
         half_lo = placed([P, 1], F32, "half_lo", 0)
         half_hi = placed([P, 1], F32, "half_hi", TILE_BYTES)
         nc.vector.memset(half_lo[:], 0.5)
         nc.vector.memset(half_hi[:], 0.5)
+        minus_half = tagged([P, 1], F32, "minus_half")
+        nc.vector.memset(minus_half[:], -0.5)
 
         xw_tab = load_words(x_words, "xw_tab")
         nc.sync.dma_start(offs_t[:], offs)
@@ -113,8 +155,10 @@ def tile_picked_zgru_gru_po_kernel(
         ew_tab = load_words(e_words, "ew_tab")
         v3_raw = load_weight(v3, tagged([P, PACK, N], F32, "v3_raw"))
         w1_raw = load_weight(w1, tagged([P, PACK, N], F32, "w1_raw"))
+        carries = {t: load_carry(t) for t in (1, 0)}
         v1_raw = load_weight(v1, tagged([P, PACK, N], F32, "v1_raw"))
-        carries = [load_carry(t) for t in range(PACK)]
+        for t in range(2, PACK):
+            carries[t] = load_carry(t)
 
         x_words_g = tagged([P, S], U32, "x_words_g")
         x_scales_g = tagged([P, S], U8, "x_scales_g")
@@ -123,17 +167,19 @@ def tile_picked_zgru_gru_po_kernel(
         x_picked = (x_words_g[:], x_scales_g[:])
         w2_lo = round_weight(nc.vector.tensor_copy, w2_raw, 0, 2, tagged([P, 2 * N], BF16, "w2_lo"))
         w2_hi = round_weight(nc.scalar.copy, w2_raw, 2, 4, tagged([P, 2 * N], BF16, "w2_hi"))
-        w2_q = quantise(w2_lo, "w2_lo") + quantise(w2_hi, "w2_hi")
+        w2_q = [quantise(w2_lo, "w2_lo"), quantise(w2_hi, "w2_hi")]
         e_scales_g = tagged([P, S], U8, "e_scales_g", "xs_tab")
         nc.vector.tensor_copy(e_scales_g[:], es_tab[:].indirect(tok_t[:]))
         r_ps = banks(0, "r_ps")
-        product(r_ps, w2_q, x_picked, True, True)
+        half_product(r_ps, 0, w2_q[0], x_picked)
+        half_product(r_ps, 1, w2_q[1], x_picked)
 
         w3_lo = round_weight(nc.vector.tensor_copy, w3_raw, 0, 2, tagged([P, 2 * N], BF16, "w3_lo"))
         w3_hi = round_weight(nc.scalar.copy, w3_raw, 2, 4, tagged([P, 2 * N], BF16, "w3_hi", "w2_lo"))
-        w3_q = quantise(w3_lo, "w3_lo") + quantise(w3_hi, "w3_hi")
+        w3_q = [quantise(w3_lo, "w3_lo"), quantise(w3_hi, "w3_hi")]
         wx_ps = banks(PACK, "wx_ps")
-        product(wx_ps, w3_q, x_picked, True, True)
+        half_product(wx_ps, 0, w3_q[0], x_picked)
+        half_product(wx_ps, 1, w3_q[1], x_picked)
 
         tanh_r = [tagged([P, S], F32, "tanh_r0")]
         tanh_r.extend(placed([P, S], F32, "tanh_r%d" % t, W3_AT + TILE_BYTES * t) for t in range(1, PACK))
@@ -154,35 +200,52 @@ def tile_picked_zgru_gru_po_kernel(
         v3_hi = round_weight(nc.scalar.copy, v3_raw, 2, 4, placed([P, 2 * N], BF16, "v3_hi", TILE_BYTES))
         for t in range(PACK - 1):
             reset(t)
-        v3_q = quantise(v3_lo, "v3_lo")
-        reset(PACK - 1)
-        v3_q = v3_q + quantise(v3_hi, "v3_hi")
+        g_ps = psum.tile([P, S], F32, name="g_ps", tag="bank%d" % PACK)
+        turn_back(g_ps, twice_rwx[0], True)
         ve_ps = banks(0, "ve_ps")
-        product(ve_ps, v3_q, e_picked, True, True)
+        half_product(ve_ps, 0, quantise(v3_lo, "v3_lo"), e_picked)
+        reset(PACK - 1)
+        half_product(ve_ps, 1, quantise(v3_hi, "v3_hi"), e_picked)
 
-        w1_g = round_weight(nc.scalar.copy, w1_raw, 0, 4, tagged([P, PACK * N], BF16, "w1_g", "tanh_r0"))
-        g_arg = [tagged([P, S], F32, "g_arg%d" % t) for t in range(PACK)]
-        for t in range(PACK):
-            nc.vector.scalar_tensor_tensor(g_arg[t][:], twice_rwx[t][:], 0.5, ve_ps[t][:], MULT, ADD)
-        w1_q = quantise(w1_g, "w1", "twice_rwx2")
-        z_ps = banks(PACK, "z_ps")
-        product(z_ps, w1_q, x_picked, True, False)
-        g = tagged([P, PACK, S], F32, "g")
-        for t in range(PACK):
-            nc.scalar.activation(g[:, t, :], g_arg[t][:], TANH)
+        twice_ve = placed([P, S], F32, "twice_ve", VE_AT)
+        nc.scalar.activation(twice_ve[:], ve_ps[0][:], COPY, scale=2.0)
+        turn_back(g_ps, twice_ve, False)
+        g_arg = {i: tagged([P, S], F32, "g_arg%d" % i) for i in range(1, PACK)}
+        for i in range(1, PACK):
+            nc.vector.scalar_tensor_tensor(g_arg[i][:], twice_rwx[i][:], 0.5, ve_ps[i][:], MULT, ADD)
+        def scaled_copy(factor):
+            return lambda dst, src: nc.scalar.activation(dst, src, COPY, scale=factor)
 
-        v1_lo = round_weight(nc.scalar.copy, v1_raw, 0, 2, tagged([P, 2 * N], BF16, "v1_lo", "g_arg2"))
+        w1_lo = round_weight(scaled_copy(-0.5), w1_raw, 0, 2, tagged([P, 2 * N], BF16, "w1_lo", "tanh_r0"))
+        w1_hi = placed([P, 2 * N], BF16, "w1_hi", TILE_BYTES)
+        nc.gpsimd.tensor_copy(
+            w1_hi[:].rearrange("p (t m j) -> p m t j", t=2, j=PACK),
+            w1_raw[:].rearrange("p j (m t) -> p m t j", t=PACK)[:, :, 2:4, :],
+        )
+        g_hi = placed([P, 2, S], F32, "g_hi", VE_AT - 3 * TILE_BYTES // 2)
+        g = [tagged([P, S], F32, "g0")[:], tagged([P, S], F32, "g1")[:], g_hi[:, 0, :], g_hi[:, 1, :]]
+        nc.scalar.activation(g[1], g_arg[1][:], TANH)
+        nc.scalar.activation(g[0], g_ps[:], TANH, scale=0.5)
+        for t in range(2, PACK):
+            nc.scalar.activation(g[t], g_arg[t][:], TANH)
+        v1_lo = round_weight(scaled_copy(minus_half[:]), v1_raw, 0, 2, tagged([P, 2 * N], BF16, "v1_lo", "g_arg2"))
         v1_hi = round_weight(nc.scalar.copy, v1_raw, 2, 4, tagged([P, 2 * N], BF16, "v1_hi", "g_arg3"))
-        diff = [tagged([P, S], F32, "diff%d" % t, "g_arg2" if t == PACK - 1 else None) for t in range(PACK)]
+        diff = [tagged([P, S], F32, "diff%d" % t, {2: "minus_half", 3: "g_arg2"}.get(t)) for t in range(PACK)]
 
         def differ(t):
-            nc.vector.tensor_tensor(diff[t][:], carries[t][:].indirect(offs_t[:]), g[:, t, :], SUB)
+            nc.vector.tensor_tensor(diff[t][:], carries[t][:].indirect(offs_t[:]), g[t], SUB)
 
-        for t in range(PACK - 1):
-            differ(t)
-        v1_q = quantise(v1_lo, "v1_lo") + quantise(v1_hi, "v1_hi")
+        w1_q = [quantise(w1_lo, "w1_lo", "twice_rwx2")]
+        differ(1)
+        differ(0)
+        w1_q.append(quantise(w1_hi, "w1_hi", "carry1"))
+        z_ps = [psum.tile([P, S], F32, name="z_ps%d" % t, tag="bank%d" % b) for t, b in enumerate((5, 6, 7, 0))]
+        product(z_ps, by_tile(w1_q), x_picked, True, False)
+        v1_q = [quantise(v1_lo, "v1_lo")]
+        differ(2)
+        v1_q.append(quantise(v1_hi, "v1_hi"))
         differ(PACK - 1)
-        product(z_ps, v1_q, e_picked, False, True)
+        product(z_ps, by_tile(v1_q), e_picked, False, True)
 
         y_codes = tagged([P, S], U32, "y_codes")
         y_scales = tagged([P, S], U8, "y_scales")
@@ -192,7 +255,7 @@ def tile_picked_zgru_gru_po_kernel(
         twice_step = tagged([P, PACK, S], F32, "twice_step")
         y = tagged([P, PACK, S], F32, "y")
         for t in range(PACK):
-            nc.scalar.activation(tanh_keep[:, t, :], z_ps[t][:], TANH, scale=-0.5)
+            nc.scalar.activation(tanh_keep[:, t, :], z_ps[t][:], TANH, scale=1.0 if t < 2 else -0.5)
 
         def blend(tiles, cols):
             for t in tiles:
@@ -200,7 +263,7 @@ def tile_picked_zgru_gru_po_kernel(
                     twice_step[:, t, cols], tanh_keep[:, t, cols], 1.0, diff[t][:, cols], ADD, MULT
                 )
             for t in tiles:
-                nc.vector.scalar_tensor_tensor(y[:, t, cols], twice_step[:, t, cols], 0.5, g[:, t, cols], MULT, ADD)
+                nc.vector.scalar_tensor_tensor(y[:, t, cols], twice_step[:, t, cols], 0.5, g[t][:, cols], MULT, ADD)
             rows = slice(tiles.start, tiles.stop)
             nc.sync.dma_start(out_rows[:, rows, cols], y[:, rows, cols])
 

from contextlib import ExitStack

import concourse.mybir as mybir
from concourse.masks import make_identity

FLOPS = 5 * 2 * 512 * 512 * 512

F32 = mybir.dt.float32
BF16 = mybir.dt.bfloat16
I32 = mybir.dt.int32
U32 = mybir.dt.uint32
U16 = mybir.dt.uint16
U8 = mybir.dt.uint8
FP8X4 = mybir.dt.float8_e4m3fn_x4
ADD = mybir.AluOpType.add
SUB = mybir.AluOpType.subtract
MULT = mybir.AluOpType.mult
TANH = mybir.ActivationFunctionType.Tanh
COPY = mybir.ActivationFunctionType.Copy

P = 128
PACK = 4
S = 512
T = 1024
N = 512
HALF = S // 2
QUARTER = S // 4
E_PLANE = 4
TILE_BYTES = 2048
VE_AT = 8 * TILE_BYTES
W3_AT = 2 * TILE_BYTES


def tile_picked_zgru_gru_po_kernel(
    tc, x_words, x_scales, e_words, e_scales, w1, v1, w2, w3, v3, carry, offs, tok, out_0, out_1, out_2
):
    nc = tc.nc
    with ExitStack() as ctx:
        lists = ctx.enter_context(tc.tile_pool(name="lists", bufs=1))
        sb = ctx.enter_context(tc.tile_pool(name="sb", bufs=1))
        laid = ctx.enter_context(tc.tile_pool(name="laid", bufs=1))
        psum = ctx.enter_context(tc.psum_pool(name="psum", bufs=1))

        offs_t = lists.tile([P, S // 16], U16, name="offs_t")
        tok_t = lists.tile([P, S // 16], U16, name="tok_t")

        def tagged(shape, dt, name, over=None):
            return sb.tile(shape, dt, name=name, tag=over or name, align_bytes=64)

        def placed(shape, dt, name, offset):
            return laid.tile(shape, dt, name=name, align_bytes=64, offset=offset)

        def load_scales(src, tab, first_row):
            for q in range(4):
                rows = slice(32 * q + first_row, 32 * q + first_row + 4)
                nc.sync.dma_start(tab[rows, :].bitcast(I32), src[0, 4 * q : 4 * q + 4, :].bitcast(I32))

        def load_words(src, name):
            tab = tagged([P, T], I32, name)
            nc.sync.dma_start(tab[:], src[0].rearrange("p n t -> p (n t)").bitcast(I32))
            return tab

        def load_weight(w, raw):
            nc.sync.dma_start(raw[:], w.rearrange("(p j) c -> p j c", j=PACK))
            return raw

        def load_carry(t):
            tab = tagged([P, T], F32, "carry%d" % t)
            nc.sync.dma_start(tab[:], carry.rearrange("(p t) c -> p t c", t=PACK)[:, t, :])
            return tab

        def round_weight(copy, raw, t0, t1, grouped):
            src = raw[:].rearrange("p j (m t) -> p m j t", t=PACK)[:, :, :, t0:t1]
            copy(grouped[:].rearrange("p (t m j) -> p m j t", t=t1 - t0, j=PACK), src)
            return grouped

        def quantise(grouped, name, over=None):
            width = grouped.shape[1] // PACK
            codes = tagged([P, width], U32, name + "_codes", over)
            scales = tagged([P, width], U8, name + "_scales")
            nc.vector.quantize_mx(out=codes[:].bitcast(FP8X4), scales=scales[:], in_=grouped[:])
            return codes, scales

        def by_tile(halves):
            return [(codes[:, c : c + P], scales[:, c : c + P]) for codes, scales in halves for c in range(0, codes.shape[1], P)]

        def banks(first, name):
            return [psum.tile([P, S], F32, name="%s%d" % (name, t), tag="bank%d" % (first + t)) for t in range(PACK)]

        def product(acc, weight, picked, start, stop):
            for t in range(PACK):
                nc.tensor.matmul_mx(
                    out=acc[t][:],
                    lhsT=weight[t][0].bitcast(FP8X4),
                    lhsT_scale=weight[t][1],
                    rhs=picked[0].bitcast(FP8X4),
                    rhs_scale=picked[1],
                    start=start,
                    stop=stop,
                )

        def mx_pass(out, stationary, moving):
            nc.tensor.matmul_mx(
                out=out,
                lhsT=stationary[0].bitcast(FP8X4),
                lhsT_scale=stationary[1],
                rhs=moving[0].bitcast(FP8X4),
                rhs_scale=moving[1],
                start=True,
                stop=True,
            )

        def half_product(acc, h, half, picked):
            for t, tile in enumerate(by_tile([half]), 2 * h):
                if t:
                    mx_pass(acc[t][:], tile, picked)
                    continue
                for u in range(PACK):
                    cols = slice(P * u, P * (u + 1))
                    mx_pass(acc[0][:, cols], (picked[0][:, cols], picked[1][:, cols]), tile)

        def turn_back(acc, src, first):
            for u in range(PACK):
                cols = slice(P * u, P * (u + 1))
                nc.tensor.matmul(
                    acc[:, cols],
                    lhsT=src[:, cols],
                    rhs=ident[:],
                    is_transpose=True,
                    start=first and u == 0,
                    stop=not first and u == PACK - 1,
                )

        xs_tab = tagged([P, T], U8, "xs_tab")
        es_tab = tagged([P, T], U8, "es_tab")
        nc.gpsimd.memset(xs_tab[:].bitcast(I32), 0)
        nc.vector.memset(es_tab[:].bitcast(I32), 0)
        ident = tagged([P, P], F32, "ident")
        make_identity(nc, ident[:])

        half_lo = placed([P, 1], F32, "half_lo", 0)
        half_hi = placed([P, 1], F32, "half_hi", TILE_BYTES)
        nc.vector.memset(half_lo[:], 0.5)
        nc.vector.memset(half_hi[:], 0.5)
        minus_half = tagged([P, 1], F32, "minus_half")
        nc.vector.memset(minus_half[:], -0.5)

        xw_tab = load_words(x_words, "xw_tab")
        nc.sync.dma_start(offs_t[:], offs)
        load_scales(x_scales, xs_tab, 0)
        nc.sync.dma_start(tok_t[:], tok)
        w2_raw = load_weight(w2, tagged([P, PACK, N], F32, "w2_raw"))
        load_scales(e_scales, es_tab, E_PLANE)
        w3_raw = load_weight(w3, placed([P, PACK, N], F32, "w3_raw", W3_AT))
        ew_tab = load_words(e_words, "ew_tab")
        v3_raw = load_weight(v3, tagged([P, PACK, N], F32, "v3_raw"))
        w1_raw = load_weight(w1, tagged([P, PACK, N], F32, "w1_raw"))
        carries = {t: load_carry(t) for t in (1, 0)}
        v1_raw = load_weight(v1, tagged([P, PACK, N], F32, "v1_raw"))
        for t in range(2, PACK):
            carries[t] = load_carry(t)

        x_words_g = tagged([P, S], U32, "x_words_g")
        x_scales_g = tagged([P, S], U8, "x_scales_g")
        nc.vector.tensor_copy(x_words_g[:], xw_tab[:].bitcast(U32).indirect(offs_t[:]))
        nc.vector.tensor_copy(x_scales_g[:], xs_tab[:].indirect(offs_t[:]))
        x_picked = (x_words_g[:], x_scales_g[:])
        w2_lo = round_weight(nc.vector.tensor_copy, w2_raw, 0, 2, tagged([P, 2 * N], BF16, "w2_lo"))
        w2_hi = round_weight(nc.scalar.copy, w2_raw, 2, 4, tagged([P, 2 * N], BF16, "w2_hi"))
        w2_q = [quantise(w2_lo, "w2_lo"), quantise(w2_hi, "w2_hi")]
        e_scales_g = tagged([P, S], U8, "e_scales_g", "xs_tab")
        nc.vector.tensor_copy(e_scales_g[:], es_tab[:].indirect(tok_t[:]))
        r_ps = banks(0, "r_ps")
        half_product(r_ps, 0, w2_q[0], x_picked)
        half_product(r_ps, 1, w2_q[1], x_picked)

        w3_lo = round_weight(nc.vector.tensor_copy, w3_raw, 0, 2, tagged([P, 2 * N], BF16, "w3_lo"))
        w3_hi = round_weight(nc.scalar.copy, w3_raw, 2, 4, tagged([P, 2 * N], BF16, "w3_hi", "w2_lo"))
        w3_q = [quantise(w3_lo, "w3_lo"), quantise(w3_hi, "w3_hi")]
        wx_ps = banks(PACK, "wx_ps")
        half_product(wx_ps, 0, w3_q[0], x_picked)
        half_product(wx_ps, 1, w3_q[1], x_picked)

        tanh_r = [tagged([P, S], F32, "tanh_r0")]
        tanh_r.extend(placed([P, S], F32, "tanh_r%d" % t, W3_AT + TILE_BYTES * t) for t in range(1, PACK))
        for t in range(PACK):
            half = half_lo if t < PACK - 1 else half_hi
            nc.scalar.activation(tanh_r[t][:], r_ps[t][:], TANH, scale=half[:])
        e_words_g = tagged([P, S], U32, "e_words_g", "w3_lo")
        nc.vector.tensor_copy(e_words_g[:], ew_tab[:].bitcast(U32).indirect(tok_t[:]))
        e_picked = (e_words_g[:], e_scales_g[E_PLANE:P, :])

        twice_rwx = [tagged([P, S], F32, "twice_rwx%d" % t) for t in range(PACK - 1)]
        twice_rwx.append(placed([P, S], F32, "twice_rwx3", 0))

        def reset(t):
            nc.vector.scalar_tensor_tensor(twice_rwx[t][:], tanh_r[t][:], 1.0, wx_ps[t][:], ADD, MULT)

        v3_lo = round_weight(nc.scalar.copy, v3_raw, 0, 2, placed([P, 2 * N], BF16, "v3_lo", 0))
        v3_hi = round_weight(nc.scalar.copy, v3_raw, 2, 4, placed([P, 2 * N], BF16, "v3_hi", TILE_BYTES))
        for t in range(PACK - 1):
            reset(t)
        g_ps = psum.tile([P, S], F32, name="g_ps", tag="bank%d" % PACK)
        turn_back(g_ps, twice_rwx[0], True)
        ve_ps = banks(0, "ve_ps")
        half_product(ve_ps, 0, quantise(v3_lo, "v3_lo"), e_picked)
        reset(PACK - 1)
        half_product(ve_ps, 1, quantise(v3_hi, "v3_hi"), e_picked)

        twice_ve = placed([P, S], F32, "twice_ve", VE_AT)
        nc.scalar.activation(twice_ve[:], ve_ps[0][:], COPY, scale=2.0)
        turn_back(g_ps, twice_ve, False)
        g_arg = {i: tagged([P, S], F32, "g_arg%d" % i) for i in range(1, PACK)}
        for i in range(1, PACK):
            nc.vector.scalar_tensor_tensor(g_arg[i][:], twice_rwx[i][:], 0.5, ve_ps[i][:], MULT, ADD)
        def scaled_copy(factor):
            return lambda dst, src: nc.scalar.activation(dst, src, COPY, scale=factor)

        w1_lo = round_weight(scaled_copy(-0.5), w1_raw, 0, 2, tagged([P, 2 * N], BF16, "w1_lo", "tanh_r0"))
        w1_hi = placed([P, 2 * N], BF16, "w1_hi", TILE_BYTES)
        nc.gpsimd.tensor_copy(
            w1_hi[:].rearrange("p (t m j) -> p m t j", t=2, j=PACK),
            w1_raw[:].rearrange("p j (m t) -> p m t j", t=PACK)[:, :, 2:4, :],
        )
        g_hi = placed([P, 2, S], F32, "g_hi", VE_AT - 3 * TILE_BYTES // 2)
        g = [tagged([P, S], F32, "g0")[:], tagged([P, S], F32, "g1")[:], g_hi[:, 0, :], g_hi[:, 1, :]]
        nc.scalar.activation(g[1], g_arg[1][:], TANH)
        nc.scalar.activation(g[0], g_ps[:], TANH, scale=0.5)
        for t in range(2, PACK):
            nc.scalar.activation(g[t], g_arg[t][:], TANH)
        v1_lo = round_weight(scaled_copy(minus_half[:]), v1_raw, 0, 2, tagged([P, 2 * N], BF16, "v1_lo", "g_arg2"))
        v1_hi = round_weight(nc.scalar.copy, v1_raw, 2, 4, tagged([P, 2 * N], BF16, "v1_hi", "g_arg3"))
        diff = [tagged([P, S], F32, "diff%d" % t, {2: "minus_half", 3: "g_arg2"}.get(t)) for t in range(PACK)]

        def differ(t):
            nc.vector.tensor_tensor(diff[t][:], carries[t][:].indirect(offs_t[:]), g[t], SUB)

        w1_q = [quantise(w1_lo, "w1_lo", "twice_rwx2")]
        differ(1)
        differ(0)
        w1_q.append(quantise(w1_hi, "w1_hi", "carry1"))
        z_ps = [psum.tile([P, S], F32, name="z_ps%d" % t, tag="bank%d" % b) for t, b in enumerate((5, 6, 7, 0))]
        product(z_ps, by_tile(w1_q), x_picked, True, False)
        v1_q = [quantise(v1_lo, "v1_lo")]
        differ(2)
        v1_q.append(quantise(v1_hi, "v1_hi"))
        differ(PACK - 1)
        product(z_ps, by_tile(v1_q), e_picked, False, True)

        y_codes = tagged([P, S], U32, "y_codes")
        y_scales = tagged([P, S], U8, "y_scales")
        out_rows = out_0.rearrange("(p t) c -> p t c", t=PACK)
        out_words = out_1[0].rearrange("p n t -> p (n t)").bitcast(I32)
        tanh_keep = tagged([P, PACK, S], F32, "tanh_keep")
        twice_step = tagged([P, PACK, S], F32, "twice_step")
        y = tagged([P, PACK, S], F32, "y")
        for t in range(PACK):
            nc.scalar.activation(tanh_keep[:, t, :], z_ps[t][:], TANH, scale=1.0 if t < 2 else -0.5)

        def blend(tiles, cols):
            for t in tiles:
                nc.vector.scalar_tensor_tensor(
                    twice_step[:, t, cols], tanh_keep[:, t, cols], 1.0, diff[t][:, cols], ADD, MULT
                )
            for t in tiles:
                nc.vector.scalar_tensor_tensor(y[:, t, cols], twice_step[:, t, cols], 0.5, g[t][:, cols], MULT, ADD)
            rows = slice(tiles.start, tiles.stop)
            nc.sync.dma_start(out_rows[:, rows, cols], y[:, rows, cols])

        def round_result(copy, cols, name):
            grouped = tagged([P, cols.stop - cols.start, PACK], BF16, name)
            copy(
                grouped[:].rearrange("p (c i) t -> p c t i", i=4),
                y[:, :, cols].rearrange("p t (c i) -> p c t i", i=4),
            )
            return grouped

        def quantise_result(grouped, cols):
            nc.vector.quantize_mx(
                out=y_codes[:, cols].bitcast(FP8X4), scales=y_scales[:, cols], in_=grouped[:].rearrange("p c t -> p (c t)")
            )

        left, right = slice(0, HALF), slice(HALF, S)
        third, fourth = slice(HALF, HALF + QUARTER), slice(HALF + QUARTER, S)
        blend(range(0, 2), slice(0, S))
        blend(range(2, PACK), left)
        y_left = round_result(nc.scalar.copy, left, "y_left")
        blend(range(2, PACK), right)
        quantise_result(y_left, left)
        nc.sync.dma_start(out_words[:, left], y_codes[:, left].bitcast(I32))
        y_third = round_result(nc.vector.tensor_copy, third, "y_third")
        y_fourth = round_result(nc.scalar.copy, fourth, "y_fourth")
        quantise_result(y_third, third)
        quantise_result(y_fourth, fourth)
        nc.sync.dma_start(out_words[:, right], y_codes[:, right].bitcast(I32))
        for q in range(4):
            queue = nc.scalar if q % 2 else nc.sync
            queue.dma_start(out_2[0, 4 * q : 4 * q + 4, :].bitcast(I32), y_scales[32 * q : 32 * q + 4, :].bitcast(I32))
